import numpy as np
import ml_dtypes


def mxq(x, axis, fmt="e4m3"):
    dtype, down = {"e4m3": (ml_dtypes.float8_e4m3fn, 7), "e5m2": (ml_dtypes.float8_e5m2, 14)}[fmt]
    v = np.moveaxis(np.asarray(x, np.float32).astype(ml_dtypes.bfloat16).astype(np.float64), axis, -1)
    blocks = v.reshape(v.shape[:-1] + (-1, 32))
    amax = np.abs(blocks).max(-1, keepdims=True)
    byte = np.maximum(np.where(amax > 0, np.frexp(amax)[1] - 1 + 127, 0) - down, 1)
    scale = np.exp2(byte - 127.0)
    codes = (blocks / scale).astype(np.float32).astype(dtype).astype(np.float64)
    return np.moveaxis((codes * scale).reshape(v.shape), -1, axis)


WIDE = False


def mx_kscale(k):
    if not WIDE:
        return np.ones(k)
    levels = np.array([10, -10, 5, -5, 0])
    if k % 512:
        return np.exp2(np.random.permutation(np.resize(levels, k // 32))).repeat(32)
    a = np.empty((k // 512, 16))
    for p in range(k // 512):
        a[p, :8] = np.random.permutation(np.resize(levels, 8))
        for g in range(8):
            far = levels[np.abs(levels - a[p, g]) >= 10]
            a[p, g + 8] = far[np.random.randint(len(far))]
    return np.exp2(a.ravel()).repeat(32)


def f64(x):
    return np.asarray(x).astype(np.float64)


def striped(idx):
    return np.tile(np.asarray(idx).reshape(-1, 16).T, (8, 1)).astype(np.uint16)


def unstriped(offs):
    return offs[:16].T.reshape(-1).astype(np.int64)


E2M1 = np.array([0.0, 0.5, 1.0, 1.5, 2.0, 3.0, 4.0, 6.0, -0.0, -0.5, -1.0, -1.5, -2.0, -3.0, -4.0, -6.0])


def pack_weight(w, fmt):
    k, n = w.shape
    w = f64(np.asarray(w, np.float32).astype(ml_dtypes.bfloat16)).reshape(k // 32, 32, n)
    amax = np.abs(w).max(1)
    if fmt == "e4m3":
        byte = np.frexp(amax)[1] - 1 + 127 - 7
    else:
        mant, ex = np.frexp(amax / 6.0)
        byte = np.where(mant > 0.5, ex, ex - 1) + 127
    byte = np.clip(np.where(amax > 0, byte, 1), 1, 254)
    scaled = (w * np.exp2(127.0 - byte)[:, None, :]).reshape(k, n).astype(np.float32)
    by_word = np.ascontiguousarray(scaled.reshape(k // 512, 128, 4, n).transpose(0, 1, 3, 2))
    if fmt == "e4m3":
        words = by_word.astype(ml_dtypes.float8_e4m3fn).view(np.uint8)
    else:
        c = by_word.astype(ml_dtypes.float4_e2m1fn).view(np.uint8) & 0xF
        words = (c[..., 0::2] | (c[..., 1::2] << 4)).reshape(k // 512, 128, 2 * n)
    return np.ascontiguousarray(words), np.ascontiguousarray(byte.astype(np.uint8).reshape(k // 512, 16, n))


def unpack_weight(words, scales, fmt):
    g, _, n = scales.shape
    words = np.ascontiguousarray(words).reshape(g, 128, n, -1)
    if fmt == "e4m3":
        vals = words.view(ml_dtypes.float8_e4m3fn).astype(np.float64)
    else:
        nib = np.empty((g, 128, n, 4), np.uint8)
        nib[..., 0::2] = words & 0xF
        nib[..., 1::2] = words >> 4
        vals = E2M1[nib]
    vals = vals * np.repeat(np.exp2(scales.astype(np.float64) - 127.0), 8, axis=1)[..., None]
    return vals.transpose(0, 1, 3, 2).reshape(g * 512, n)


B, N, T, D, NQ = 1, 512, 4096, 1024, 128


def setup_inputs():
    n = np.random.standard_normal
    idx = np.random.permutation(T)[:B * N]
    s = mx_kscale(D)[:, None]
    kp = pack_weight(n((D, T)) / s, "e2m1")
    return {
        "qT": (n((B, D, NQ)) * s * (1.00 / np.sqrt(D))).astype(np.float32),
        "k_words": np.ascontiguousarray(kp[0].reshape(1, 2, 128, T, 2).transpose(0, 2, 3, 1, 4)).reshape(1, 128, T, 4),
        "k_scales": kp[1],
        "nb": np.tile(0.5 * n(4096), (128, 1)).astype(np.float32),
        "offs": striped(idx),
    }


def reference(qT, k_words, k_scales, nb, offs):
    idx = unstriped(offs)
    pick = lambda x, which: x[:, which].reshape(x.shape[0], B, -1).transpose(1, 0, 2)
    k = unpack_weight(k_words.reshape(1, 128, T, 2, 2).transpose(0, 3, 1, 2, 4).reshape(2, 128, 2 * T), k_scales, "e2m1")
    kg = pick(k, idx)
    qq = mxq(f64(qT), 1, "e4m3")
    a = qq.transpose(0, 2, 1) @ kg
    y = np.maximum(a + pick(f64(nb), idx)[:, :1, :], 0.0)
    return y

@@ -1,0 +1,142 @@
+from contextlib import ExitStack
+
+import concourse.mybir as mybir
+from concourse.masks import make_identity
+
+D, NQ, T, N = 1024, 128, 4096, 512
+FLOPS = 2 * D * NQ * N
+BYTES = D * NQ * 4 + 128 * T * 4 + 32 * T + T * 4 + 128 * 32 * 2 + NQ * N * 4
+
+F32 = mybir.dt.float32
+BF16 = mybir.dt.bfloat16
+I32 = mybir.dt.int32
+U32 = mybir.dt.uint32
+U16 = mybir.dt.uint16
+U8 = mybir.dt.uint8
+FP8X4 = mybir.dt.float8_e4m3fn_x4
+FP4X4 = mybir.dt.float4_e2m1fn_x4
+ACT = mybir.ActivationFunctionType
+ALU = mybir.AluOpType
+
+P = 128
+PACK = 4
+PASSES = 2
+CH = 128
+NCH = N // CH
+BIAS_ROW = P - 1
+
+
+def tile_attend_neu_relu_topk_kernel(tc, qT, k_words, k_scales, nb, offs, out):
+    nc = tc.nc
+    with ExitStack() as ctx:
+        sb = ctx.enter_context(tc.tile_pool(name="sb", bufs=1))
+        ps = ctx.enter_context(tc.psum_pool(name="ps", bufs=1))
+
+        offsets = sb.tile([P, N // 16], U16, name="offsets")
+        nc.sync.dma_start(offsets[:], offs)
+
+        sc_win = sb.tile([P, PASSES, T], U8, name="sc_win", align_bytes=64)
+        sc_i32 = sc_win[:].rearrange("p o t -> p (o t)").bitcast(I32)
+        nc.vector.memset(sc_i32, 0)
+        nc.scalar.dma_start(
+            sc_i32.rearrange("p (o t) -> p o t", o=PASSES)[0:P:8, :, :],
+            k_scales.rearrange("o f t -> f o t").bitcast(I32),
+        )
+
+        nb_win = sb.tile([P, T], F32, name="nb_win", align_bytes=64)
+        nc.sync.dma_start(nb_win[BIAS_ROW:P, :], nb[0:1, :])
+
+        w_win = sb.tile([P, T], I32, name="w_win", align_bytes=64)
+        nc.sync.dma_start(w_win[:], k_words[0].rearrange("p t b -> p (t b)").bitcast(I32))
+
+        q_raw = [sb.tile([P, PACK, NQ], F32, name="q_raw%d" % o) for o in range(PASSES)]
+        for o in range(PASSES):
+            nc.sync.dma_start(q_raw[o][:], qT[0, 512 * o : 512 * (o + 1), :].rearrange("(p j) w -> p j w", j=PACK))
+
+        warm = sb.tile([P, 2], F32, name="warm")
+        nc.vector.memset(warm[:, 0:1], 0.0)
+        warm2 = sb.tile([P, 2], F32, name="warm2")
+        nc.scalar.activation(warm2[:, 0:1], warm[:, 0:1], ACT.Relu)
+
+        planes = sb.tile([P, PASSES, N], U8, name="planes", align_bytes=64)
+        planes_i32 = planes[:].rearrange("p o n -> p (o n)").bitcast(I32)
+        nc.vector.memset(planes_i32, 0)
+        nc.vector.memset(nb_win[0:BIAS_ROW, :], 0.0)
+
+        ident = sb.tile([P, P], F32, name="ident")
+        make_identity(nc, ident[:])
+
+        sc_got = sb.tile([P, PASSES, N], U8, name="sc_got", align_bytes=64)
+        for o in range(PASSES):
+            nc.vector.tensor_copy(sc_got[:, o, :], sc_win[:, o, :].indirect(offsets[:]))
+        sc_got_i32 = sc_got[:].rearrange("p o n -> p (o n)").bitcast(I32)
+        for r in range(4):
+            nc.sync.dma_start(planes_i32[r:P:32, :], sc_got_i32[8 * r : P : 32, :])
+
+        nb_got = sb.tile([P, N], F32, name="nb_got", align_bytes=64)
+        nc.vector.tensor_copy(nb_got[:], nb_win[:].indirect(offsets[:]))
+
+        w_got = sb.tile([P, N], U32, name="w_got", align_bytes=64)
+        nc.vector.tensor_copy(w_got[:], w_win[:].bitcast(U32).indirect(offsets[:]))
+
+        turned = ps.tile([P, NCH, CH], F32, name="turned")
+        for c in range(NCH):
+            nc.tensor.transpose(turned[:, c, :], nb_got[:, c * CH : (c + 1) * CH], ident[:])
+        nb_col = sb.tile([P, NCH], F32, name="nb_col")
+        nc.scalar.copy(nb_col[:], turned[:, :, BIAS_ROW])
+        spread = ps.tile([P, N], F32, name="spread")
+        for c in range(NCH):
+            nc.tensor.transpose(spread[:, c * CH : (c + 1) * CH], nb_col[:, c : c + 1].to_broadcast([P, P]), ident[:])
+
+        q_bf = [sb.tile([P, NQ, PACK], BF16, name="q_bf%d" % o, align_bytes=64) for o in range(PASSES)]
+        q_codes = [sb.tile([P, NQ], U32, name="q_codes%d" % o, align_bytes=64) for o in range(PASSES)]
+        q_scales = [sb.tile([P, NQ], U8, name="q_scales%d" % o, align_bytes=64) for o in range(PASSES)]
+        for o in range(PASSES):
+            nc.scalar.copy(
+                q_bf[o][:].rearrange("p (c i) t -> p c t i", i=4),
+                q_raw[o][:].rearrange("p t (c i) -> p c t i", i=4),
+            )
+        bias = sb.tile([P, N], F32, name="bias")
+        nc.scalar.copy(bias[:], spread[:])
+
+        keys = [sb.tile([P, PASSES, 2 * CH], U8, name="keys%d" % c, align_bytes=64) for c in range(NCH)]
+        halves = w_got[:].bitcast(U16).rearrange("p (n h) -> p h n", h=PASSES)
+
+        def split(c):
+            nc.vector.tensor_copy(keys[c][:].bitcast(U16), halves[:, :, c * CH : (c + 1) * CH])
+
+        def quantize(o):
+            nc.vector.quantize_mx(
+                out=q_codes[o][:].bitcast(FP8X4),
+                scales=q_scales[o][:],
+                in_=q_bf[o][:].rearrange("p w j -> p (w j)"),
+            )
+
+        split(0)
+        quantize(0)
+        split(1)
+        split(2)
+        split(3)
+        quantize(1)
+
+        acc = [ps.tile([P, CH], F32, name="acc%d" % c) for c in range(NCH)]
+        for o in range(PASSES):
+            for c in range(NCH):
+                nc.tensor.matmul_mx(
+                    out=acc[c][:],
+                    lhsT=q_codes[o][:].bitcast(FP8X4),
+                    lhsT_scale=q_scales[o][:],
+                    rhs=keys[c][:, o, :].bitcast(FP4X4),
+                    rhs_scale=planes[:, o, c * CH : (c + 1) * CH],
+                    start=(o == 0),
+                    stop=(o == PASSES - 1),
+                )
+
+        res = [sb.tile([P, 2 * CH], F32, name="res%d" % h) for h in range(2)]
+        for c in range(NCH):
+            summed = sb.tile([P, CH], F32, name="summed%d" % c)
+            nc.vector.tensor_tensor(summed[:], acc[c][:], bias[:, c * CH : (c + 1) * CH], ALU.add)
+            nc.scalar.activation(res[c // 2][:, (c % 2) * CH : (c % 2 + 1) * CH], summed[:], ACT.Relu)
+            if c % 2 == 1:
+                h = c // 2
+                nc.sync.dma_start(out[0, :, h * 2 * CH : (h + 1) * 2 * CH], res[h][:])

@@ -35,46 +35,34 @@ def tile_attend_neu_relu_topk_kernel(tc, qT, k_words, k_scales, nb, offs, out):
         offsets = sb.tile([P, N // 16], U16, name="offsets")
         nc.sync.dma_start(offsets[:], offs)
 
-        sc_win = sb.tile([P, PASSES, T], U8, name="sc_win", align_bytes=64)
-        sc_i32 = sc_win[:].rearrange("p o t -> p (o t)").bitcast(I32)
-        nc.vector.memset(sc_i32, 0)
-        nc.scalar.dma_start(
-            sc_i32.rearrange("p (o t) -> p o t", o=PASSES)[0:P:8, :, :],
-            k_scales.rearrange("o f t -> f o t").bitcast(I32),
-        )
-
         nb_win = sb.tile([P, T], F32, name="nb_win", align_bytes=64)
         nc.sync.dma_start(nb_win[BIAS_ROW:P, :], nb[0:1, :])
-
+        sc_win = sb.tile([P, T], U8, name="sc_win", align_bytes=64)
+        sc_i32 = sc_win[:].bitcast(I32)
+        nc.sync.dma_start(sc_i32[0:32, :], k_scales.rearrange("o f t -> f o t").bitcast(I32))
         w_win = sb.tile([P, T], I32, name="w_win", align_bytes=64)
         nc.sync.dma_start(w_win[:], k_words[0].rearrange("p t b -> p (t b)").bitcast(I32))
-
         q_raw = [sb.tile([P, PACK, NQ], F32, name="q_raw%d" % o) for o in range(PASSES)]
         for o in range(PASSES):
             nc.sync.dma_start(q_raw[o][:], qT[0, 512 * o : 512 * (o + 1), :].rearrange("(p j) w -> p j w", j=PACK))
 
-        warm = sb.tile([P, 2], F32, name="warm")
-        nc.vector.memset(warm[:, 0:1], 0.0)
-        warm2 = sb.tile([P, 2], F32, name="warm2")
-        nc.scalar.activation(warm2[:, 0:1], warm[:, 0:1], ACT.Relu)
-
-        planes = sb.tile([P, PASSES, N], U8, name="planes", align_bytes=64)
-        planes_i32 = planes[:].rearrange("p o n -> p (o n)").bitcast(I32)
-        nc.vector.memset(planes_i32, 0)
         nc.vector.memset(nb_win[0:BIAS_ROW, :], 0.0)
-
+        nc.vector.memset(sc_i32[32:64, :], 0)
+        nc.vector.memset(sc_i32[64:P, :], 0)
         ident = sb.tile([P, P], F32, name="ident")
-        make_identity(nc, ident[:])
-
-        sc_got = sb.tile([P, PASSES, N], U8, name="sc_got", align_bytes=64)
-        for o in range(PASSES):
-            nc.vector.tensor_copy(sc_got[:, o, :], sc_win[:, o, :].indirect(offsets[:]))
-        sc_got_i32 = sc_got[:].rearrange("p o n -> p (o n)").bitcast(I32)
-        for r in range(4):
-            nc.sync.dma_start(planes_i32[r:P:32, :], sc_got_i32[8 * r : P : 32, :])
+        nc.vector.memset(ident[:], 0.0)
+        make_identity(nc, ident[:], nomemset=True)
 
         nb_got = sb.tile([P, N], F32, name="nb_got", align_bytes=64)
         nc.vector.tensor_copy(nb_got[:], nb_win[:].indirect(offsets[:]))
+
+        planes = sb.tile([P, PASSES, N], U8, name="planes", align_bytes=64)
+        planes_i32 = planes[:].bitcast(I32)
+        sc_got = sb.tile([P, N], U8, name="sc_got", align_bytes=64)
+        nc.vector.tensor_copy(sc_got[:], sc_win[:].indirect(offsets[:]))
+        sc_got_i32 = sc_got[:].bitcast(I32)
+        for quad in range(4):
+            nc.sync.dma_start(planes_i32[32 * quad : 32 * quad + 4, :, :], sc_got_i32[8 * quad : 8 * quad + 8, :])
 
         w_got = sb.tile([P, N], U32, name="w_got", align_bytes=64)
         nc.vector.tensor_copy(w_got[:], w_win[:].bitcast(U32).indirect(offsets[:]))
@@ -88,6 +76,9 @@ def tile_attend_neu_relu_topk_kernel(tc, qT, k_words, k_scales, nb, offs, out):
         for c in range(NCH):
             nc.tensor.transpose(spread[:, c * CH : (c + 1) * CH], nb_col[:, c : c + 1].to_broadcast([P, P]), ident[:])
 
+        bias = sb.tile([P, N], F32, name="bias")
+        nc.scalar.copy(bias[:], spread[:])
+
         q_bf = [sb.tile([P, NQ, PACK], BF16, name="q_bf%d" % o, align_bytes=64) for o in range(PASSES)]
         q_codes = [sb.tile([P, NQ], U32, name="q_codes%d" % o, align_bytes=64) for o in range(PASSES)]
         q_scales = [sb.tile([P, NQ], U8, name="q_scales%d" % o, align_bytes=64) for o in range(PASSES)]
@@ -96,14 +87,6 @@ def tile_attend_neu_relu_topk_kernel(tc, qT, k_words, k_scales, nb, offs, out):
                 q_bf[o][:].rearrange("p (c i) t -> p c t i", i=4),
                 q_raw[o][:].rearrange("p t (c i) -> p c t i", i=4),
             )
-        bias = sb.tile([P, N], F32, name="bias")
-        nc.scalar.copy(bias[:], spread[:])
-
-        keys = [sb.tile([P, PASSES, 2 * CH], U8, name="keys%d" % c, align_bytes=64) for c in range(NCH)]
-        halves = w_got[:].bitcast(U16).rearrange("p (n h) -> p h n", h=PASSES)
-
-        def split(c):
-            nc.vector.tensor_copy(keys[c][:].bitcast(U16), halves[:, :, c * CH : (c + 1) * CH])
 
         def quantize(o):
             nc.vector.quantize_mx(
@@ -112,11 +95,16 @@ def tile_attend_neu_relu_topk_kernel(tc, qT, k_words, k_scales, nb, offs, out):
                 in_=q_bf[o][:].rearrange("p w j -> p (w j)"),
             )
 
+        keys = [sb.tile([P, PASSES, 2 * CH], U8, name="keys%d" % c, align_bytes=64) for c in range(NCH)]
+        halves = w_got[:].bitcast(U16).rearrange("p (n h) -> p h n", h=PASSES)
+
+        def split(c):
+            nc.vector.tensor_copy(keys[c][:].bitcast(U16), halves[:, :, c * CH : (c + 1) * CH])
+
         split(0)
         quantize(0)
-        split(1)
-        split(2)
-        split(3)
+        for c in range(1, NCH):
+            split(c)
         quantize(1)
 
         acc = [ps.tile([P, CH], F32, name="acc%d" % c) for c in range(NCH)]
@@ -132,11 +120,15 @@ def tile_attend_neu_relu_topk_kernel(tc, qT, k_words, k_scales, nb, offs, out):
                     stop=(o == PASSES - 1),
                 )
 
-        res = [sb.tile([P, 2 * CH], F32, name="res%d" % h) for h in range(2)]
+        res = sb.tile([P, N], F32, name="res")
         for c in range(NCH):
+            cols = slice(c * CH, (c + 1) * CH)
             summed = sb.tile([P, CH], F32, name="summed%d" % c)
-            nc.vector.tensor_tensor(summed[:], acc[c][:], bias[:, c * CH : (c + 1) * CH], ALU.add)
-            nc.scalar.activation(res[c // 2][:, (c % 2) * CH : (c % 2 + 1) * CH], summed[:], ACT.Relu)
-            if c % 2 == 1:
-                h = c // 2
-                nc.sync.dma_start(out[0, :, h * 2 * CH : (h + 1) * 2 * CH], res[h][:])
+            nc.vector.tensor_tensor(summed[:], acc[c][:], bias[:, cols], ALU.add)
+            nc.scalar.activation(res[:, cols], summed[:], ACT.Relu)
+            if c == 1:
+                nc.sync.dma_start(out[0, :, 0 : 2 * CH], res[:, 0 : 2 * CH])
+            if c == 2:
+                nc.sync.dma_start(out[0, :, cols], res[:, cols])
+            if c == 3:
+                nc.scalar.dma_start(out[0, :, cols], res[:, cols])

@@ -46,12 +46,13 @@ def tile_attend_neu_relu_topk_kernel(tc, qT, k_words, k_scales, nb, offs, out):
         for o in range(PASSES):
             nc.sync.dma_start(q_raw[o][:], qT[0, 512 * o : 512 * (o + 1), :].rearrange("(p j) w -> p j w", j=PACK))
 
-        nc.vector.memset(nb_win[0:BIAS_ROW, :], 0.0)
-        nc.vector.memset(sc_i32[32:64, :], 0)
-        nc.vector.memset(sc_i32[64:P, :], 0)
+        nc.vector.memset(nb_win[0:BIAS_ROW, 0:1471], 0.0)
+        nc.vector.memset(nb_win[0:BIAS_ROW, 1471:2944], 0.0)
+        nc.gpsimd.memset(nb_win[0:BIAS_ROW, 2944:T], 0.0)
         ident = sb.tile([P, P], F32, name="ident")
-        nc.vector.memset(ident[:], 0.0)
-        make_identity(nc, ident[:], nomemset=True)
+        make_identity(nc, ident[:])
+        nc.gpsimd.memset(sc_i32[32:64, :], 0)
+        nc.gpsimd.memset(sc_i32[64:P, :], 0)
 
         nb_got = sb.tile([P, N], F32, name="nb_got", align_bytes=64)
         nc.vector.tensor_copy(nb_got[:], nb_win[:].indirect(offsets[:]))

@@ -32,25 +32,24 @@ def tile_attend_neu_relu_topk_kernel(tc, qT, k_words, k_scales, nb, offs, out):
         sb = ctx.enter_context(tc.tile_pool(name="sb", bufs=1))
         ps = ctx.enter_context(tc.psum_pool(name="ps", bufs=1))
 
-        offsets = sb.tile([P, N // 16], U16, name="offsets")
-        nc.sync.dma_start(offsets[:], offs)
-
-        nb_win = sb.tile([P, T], F32, name="nb_win", align_bytes=64)
-        nc.sync.dma_start(nb_win[BIAS_ROW:P, :], nb[0:1, :])
         sc_win = sb.tile([P, T], U8, name="sc_win", align_bytes=64)
         sc_i32 = sc_win[:].bitcast(I32)
         nc.sync.dma_start(sc_i32[0:32, :], k_scales.rearrange("o f t -> f o t").bitcast(I32))
+        nb_win = sb.tile([P, T], F32, name="nb_win", align_bytes=64)
+        nc.sync.dma_start(nb_win[BIAS_ROW:P, :], nb[0:1, :])
+        offsets = sb.tile([P, N // 16], U16, name="offsets")
+        nc.sync.dma_start(offsets[:], offs)
         w_win = sb.tile([P, T], I32, name="w_win", align_bytes=64)
         nc.sync.dma_start(w_win[:], k_words[0].rearrange("p t b -> p (t b)").bitcast(I32))
-        q_raw = [sb.tile([P, PACK, NQ], F32, name="q_raw%d" % o) for o in range(PASSES)]
+        q_raw = [sb.tile([P, PACK, NQ], F32, name="q_raw%d" % o, tag="slot%d" % o, align_bytes=64) for o in range(PASSES)]
         for o in range(PASSES):
             nc.sync.dma_start(q_raw[o][:], qT[0, 512 * o : 512 * (o + 1), :].rearrange("(p j) w -> p j w", j=PACK))
 
-        nc.vector.memset(nb_win[0:BIAS_ROW, 0:1471], 0.0)
-        nc.vector.memset(nb_win[0:BIAS_ROW, 1471:2944], 0.0)
-        nc.gpsimd.memset(nb_win[0:BIAS_ROW, 2944:T], 0.0)
         ident = sb.tile([P, P], F32, name="ident")
         make_identity(nc, ident[:])
+        nc.vector.memset(nb_win[0:BIAS_ROW, 0:1407], 0.0)
+        nc.vector.memset(nb_win[0:BIAS_ROW, 1407:2816], 0.0)
+        nc.gpsimd.memset(nb_win[0:BIAS_ROW, 2816:T], 0.0)
         nc.gpsimd.memset(sc_i32[32:64, :], 0)
         nc.gpsimd.memset(sc_i32[64:P, :], 0)
 
@@ -77,9 +76,6 @@ def tile_attend_neu_relu_topk_kernel(tc, qT, k_words, k_scales, nb, offs, out):
         for c in range(NCH):
             nc.tensor.transpose(spread[:, c * CH : (c + 1) * CH], nb_col[:, c : c + 1].to_broadcast([P, P]), ident[:])
 
-        bias = sb.tile([P, N], F32, name="bias")
-        nc.scalar.copy(bias[:], spread[:])
-
         q_bf = [sb.tile([P, NQ, PACK], BF16, name="q_bf%d" % o, align_bytes=64) for o in range(PASSES)]
         q_codes = [sb.tile([P, NQ], U32, name="q_codes%d" % o, align_bytes=64) for o in range(PASSES)]
         q_scales = [sb.tile([P, NQ], U8, name="q_scales%d" % o, align_bytes=64) for o in range(PASSES)]
@@ -89,6 +85,10 @@ def tile_attend_neu_relu_topk_kernel(tc, qT, k_words, k_scales, nb, offs, out):
                 q_raw[o][:].rearrange("p t (c i) -> p c t i", i=4),
             )
 
+        bias = sb.tile([P, N], F32, name="bias", tag="slot1", align_bytes=64)
+        for h in range(2):
+            nc.scalar.copy(bias[:, h * 2 * CH : (h + 1) * 2 * CH], spread[:, h * 2 * CH : (h + 1) * 2 * CH])
+
         def quantize(o):
             nc.vector.quantize_mx(
                 out=q_codes[o][:].bitcast(FP8X4),
@@ -96,30 +96,39 @@ def tile_attend_neu_relu_topk_kernel(tc, qT, k_words, k_scales, nb, offs, out):
                 in_=q_bf[o][:].rearrange("p w j -> p (w j)"),
             )
 
-        keys = [sb.tile([P, PASSES, 2 * CH], U8, name="keys%d" % c, align_bytes=64) for c in range(NCH)]
+        keys_first = sb.tile([P, PASSES, 2 * CH], U8, name="keys_first", align_bytes=64)
+        keys_mid = sb.tile([P, 2, PASSES, 2 * CH], U8, name="keys_mid", tag="slot0", align_bytes=64)
+        keys_last = sb.tile([P, PASSES, 2 * CH], U8, name="keys_last", align_bytes=64)
+        keys = [keys_first[:], keys_mid[:, 0, :, :], keys_mid[:, 1, :, :], keys_last[:]]
         halves = w_got[:].bitcast(U16).rearrange("p (n h) -> p h n", h=PASSES)
 
         def split(c):
-            nc.vector.tensor_copy(keys[c][:].bitcast(U16), halves[:, :, c * CH : (c + 1) * CH])
-
-        split(0)
-        quantize(0)
-        for c in range(1, NCH):
-            split(c)
-        quantize(1)
+            nc.vector.tensor_copy(keys[c].bitcast(U16), halves[:, :, c * CH : (c + 1) * CH])
 
         acc = [ps.tile([P, CH], F32, name="acc%d" % c) for c in range(NCH)]
-        for o in range(PASSES):
-            for c in range(NCH):
-                nc.tensor.matmul_mx(
-                    out=acc[c][:],
-                    lhsT=q_codes[o][:].bitcast(FP8X4),
-                    lhsT_scale=q_scales[o][:],
-                    rhs=keys[c][:, o, :].bitcast(FP4X4),
-                    rhs_scale=planes[:, o, c * CH : (c + 1) * CH],
-                    start=(o == 0),
-                    stop=(o == PASSES - 1),
-                )
+
+        def multiply(c, o):
+            nc.tensor.matmul_mx(
+                out=acc[c][:],
+                lhsT=q_codes[o][:].bitcast(FP8X4),
+                lhsT_scale=q_scales[o][:],
+                rhs=keys[c][:, o, :].bitcast(FP4X4),
+                rhs_scale=planes[:, o, c * CH : (c + 1) * CH],
+                start=(o == 0),
+                stop=(o == PASSES - 1),
+            )
+
+        split(0)
+        split(3)
+        quantize(0)
+        nc.vector.tensor_copy(
+            keys_mid[:].bitcast(U16), halves[:, :, CH : 3 * CH].rearrange("p h (c n) -> p c h n", c=2)
+        )
+        quantize(1)
+        for c in (0, 3, 1, 2):
+            multiply(c, 0)
+        for c in range(NCH):
+            multiply(c, 1)
 
         res = sb.tile([P, N], F32, name="res")
         for c in range(NCH):

@@ -30,6 +30,7 @@ def tile_attend_neu_relu_topk_kernel(tc, qT, k_words, k_scales, nb, offs, out):
     nc = tc.nc
     with ExitStack() as ctx:
         sb = ctx.enter_context(tc.tile_pool(name="sb", bufs=1))
+        shared = ctx.enter_context(tc.tile_pool(name="shared", bufs=1))
         ps = ctx.enter_context(tc.psum_pool(name="ps", bufs=1))
 
         sc_win = sb.tile([P, T], U8, name="sc_win", align_bytes=64)
@@ -41,7 +42,7 @@ def tile_attend_neu_relu_topk_kernel(tc, qT, k_words, k_scales, nb, offs, out):
         nc.sync.dma_start(offsets[:], offs)
         w_win = sb.tile([P, T], I32, name="w_win", align_bytes=64)
         nc.sync.dma_start(w_win[:], k_words[0].rearrange("p t b -> p (t b)").bitcast(I32))
-        q_raw = [sb.tile([P, PACK, NQ], F32, name="q_raw%d" % o, tag="slot%d" % o, align_bytes=64) for o in range(PASSES)]
+        q_raw = [shared.tile([P, PACK, NQ], F32, name="q_raw%d" % o, offset=2048 * o, align_bytes=64) for o in range(PASSES)]
         for o in range(PASSES):
             nc.sync.dma_start(q_raw[o][:], qT[0, 512 * o : 512 * (o + 1), :].rearrange("(p j) w -> p j w", j=PACK))
 
@@ -53,25 +54,26 @@ def tile_attend_neu_relu_topk_kernel(tc, qT, k_words, k_scales, nb, offs, out):
         nc.gpsimd.memset(sc_i32[32:64, :], 0)
         nc.gpsimd.memset(sc_i32[64:P, :], 0)
 
-        nb_got = sb.tile([P, N], F32, name="nb_got", align_bytes=64)
+        nb_got = sb.tile([P, N], F32, name="nb_got", tag="bias_then_planes", align_bytes=64)
         nc.vector.tensor_copy(nb_got[:], nb_win[:].indirect(offsets[:]))
-
-        planes = sb.tile([P, PASSES, N], U8, name="planes", align_bytes=64)
-        planes_i32 = planes[:].bitcast(I32)
         sc_got = sb.tile([P, N], U8, name="sc_got", align_bytes=64)
         nc.vector.tensor_copy(sc_got[:], sc_win[:].indirect(offsets[:]))
-        sc_got_i32 = sc_got[:].bitcast(I32)
-        for quad in range(4):
-            nc.sync.dma_start(planes_i32[32 * quad : 32 * quad + 4, :, :], sc_got_i32[8 * quad : 8 * quad + 8, :])
-
-        w_got = sb.tile([P, N], U32, name="w_got", align_bytes=64)
-        nc.vector.tensor_copy(w_got[:], w_win[:].bitcast(U32).indirect(offsets[:]))
 
         turned = ps.tile([P, NCH, CH], F32, name="turned")
         for c in range(NCH):
             nc.tensor.transpose(turned[:, c, :], nb_got[:, c * CH : (c + 1) * CH], ident[:])
         nb_col = sb.tile([P, NCH], F32, name="nb_col")
         nc.scalar.copy(nb_col[:], turned[:, :, BIAS_ROW])
+
+        planes = sb.tile([P, PASSES, N], U8, name="planes", tag="bias_then_planes", align_bytes=64)
+        planes_i32 = planes[:].bitcast(I32)
+        sc_got_i32 = sc_got[:].bitcast(I32)
+        for quad in range(4):
+            nc.scalar.dma_start(planes_i32[32 * quad : 32 * quad + 4, :, :], sc_got_i32[8 * quad : 8 * quad + 8, :])
+
+        w_got = sb.tile([P, N], U32, name="w_got", align_bytes=64)
+        nc.vector.tensor_copy(w_got[:], w_win[:].bitcast(U32).indirect(offsets[:]))
+
         spread = ps.tile([P, N], F32, name="spread")
         for c in range(NCH):
             nc.tensor.transpose(spread[:, c * CH : (c + 1) * CH], nb_col[:, c : c + 1].to_broadcast([P, P]), ident[:])
@@ -85,7 +87,7 @@ def tile_attend_neu_relu_topk_kernel(tc, qT, k_words, k_scales, nb, offs, out):
                 q_raw[o][:].rearrange("p t (c i) -> p c t i", i=4),
             )
 
-        bias = sb.tile([P, N], F32, name="bias", tag="slot1", align_bytes=64)
+        bias = shared.tile([P, N], F32, name="bias", offset=3072, align_bytes=64)
         for h in range(2):
             nc.scalar.copy(bias[:, h * 2 * CH : (h + 1) * 2 * CH], spread[:, h * 2 * CH : (h + 1) * 2 * CH])
 
@@ -96,14 +98,11 @@ def tile_attend_neu_relu_topk_kernel(tc, qT, k_words, k_scales, nb, offs, out):
                 in_=q_bf[o][:].rearrange("p w j -> p (w j)"),
             )
 
-        keys_first = sb.tile([P, PASSES, 2 * CH], U8, name="keys_first", align_bytes=64)
-        keys_mid = sb.tile([P, 2, PASSES, 2 * CH], U8, name="keys_mid", tag="slot0", align_bytes=64)
-        keys_last = sb.tile([P, PASSES, 2 * CH], U8, name="keys_last", align_bytes=64)
-        keys = [keys_first[:], keys_mid[:, 0, :, :], keys_mid[:, 1, :, :], keys_last[:]]
-        halves = w_got[:].bitcast(U16).rearrange("p (n h) -> p h n", h=PASSES)
+        keys = [shared.tile([P, 2 * N], U8, name="keys%d" % o, offset=2048 * o, align_bytes=64) for o in range(PASSES)]
+        halves = w_got[:].bitcast(U16).rearrange("p (c n h) -> p h c n", h=PASSES, c=NCH)
 
-        def split(c):
-            nc.vector.tensor_copy(keys[c].bitcast(U16), halves[:, :, c * CH : (c + 1) * CH])
+        def split(o, lo, hi):
+            nc.vector.tensor_copy(keys[o][:].bitcast(U16).rearrange("p (c n) -> p c n", c=NCH)[:, lo:hi, :], halves[:, o, lo:hi, :])
 
         acc = [ps.tile([P, CH], F32, name="acc%d" % c) for c in range(NCH)]
 
@@ -112,23 +111,21 @@ def tile_attend_neu_relu_topk_kernel(tc, qT, k_words, k_scales, nb, offs, out):
                 out=acc[c][:],
                 lhsT=q_codes[o][:].bitcast(FP8X4),
                 lhsT_scale=q_scales[o][:],
-                rhs=keys[c][:, o, :].bitcast(FP4X4),
+                rhs=keys[o][:, 2 * c * CH : 2 * (c + 1) * CH].bitcast(FP4X4),
                 rhs_scale=planes[:, o, c * CH : (c + 1) * CH],
                 start=(o == 0),
                 stop=(o == PASSES - 1),
             )
 
-        split(0)
-        split(3)
         quantize(0)
-        nc.vector.tensor_copy(
-            keys_mid[:].bitcast(U16), halves[:, :, CH : 3 * CH].rearrange("p h (c n) -> p c h n", c=2)
-        )
+        split(0, 0, 2)
+        split(0, 2, 4)
         quantize(1)
-        for c in (0, 3, 1, 2):
-            multiply(c, 0)
-        for c in range(NCH):
-            multiply(c, 1)
+        split(1, 0, 2)
+        split(1, 2, 4)
+        for o in range(PASSES):
+            for c in range(NCH):
+                multiply(c, o)
 
         res = sb.tile([P, N], F32, name="res")
         for c in range(NCH):

@@ -1,7 +1,6 @@
 from contextlib import ExitStack
 
 import concourse.mybir as mybir
-from concourse.masks import make_identity
 
 D, NQ, T, N = 1024, 128, 4096, 512
 FLOPS = 2 * D * NQ * N
@@ -37,7 +36,7 @@ def tile_attend_neu_relu_topk_kernel(tc, qT, k_words, k_scales, nb, offs, out):
         sc_i32 = sc_win[:].bitcast(I32)
         nc.sync.dma_start(sc_i32[0:32, :], k_scales.rearrange("o f t -> f o t").bitcast(I32))
         nb_win = sb.tile([P, T], F32, name="nb_win", align_bytes=64)
-        nc.sync.dma_start(nb_win[BIAS_ROW:P, :], nb[0:1, :])
+        nc.scalar.dma_start(nb_win[BIAS_ROW:P, :], nb[0:1, :])
         offsets = sb.tile([P, N // 16], U16, name="offsets")
         nc.sync.dma_start(offsets[:], offs)
         w_win = sb.tile([P, T], I32, name="w_win", align_bytes=64)
@@ -47,17 +46,29 @@ def tile_attend_neu_relu_topk_kernel(tc, qT, k_words, k_scales, nb, offs, out):
             nc.sync.dma_start(q_raw[o][:], qT[0, 512 * o : 512 * (o + 1), :].rearrange("(p j) w -> p j w", j=PACK))
 
         ident = sb.tile([P, P], F32, name="ident")
-        make_identity(nc, ident[:])
-        nc.vector.memset(nb_win[0:BIAS_ROW, 0:1407], 0.0)
-        nc.vector.memset(nb_win[0:BIAS_ROW, 1407:2816], 0.0)
-        nc.gpsimd.memset(nb_win[0:BIAS_ROW, 2816:T], 0.0)
-        nc.gpsimd.memset(sc_i32[32:64, :], 0)
+        ramp = sb.tile([P, P], F32, name="ramp")
+        nc.gpsimd.iota(ramp[:], [[1, P]], base=0, channel_multiplier=-1, allow_small_or_imprecise_dtypes=True)
+        dist = sb.tile([P, P], F32, name="dist")
+        nc.scalar.activation(dist[:], ramp[:], ACT.Abs)
+        nc.scalar.activation(ident[:], dist[:], ACT.Relu, bias=1.0, scale=-1.0)
+        nc.vector.memset(sc_i32[32:64, 0:511], 0)
+        nc.vector.memset(sc_i32[32:64, 511:1024], 0)
         nc.gpsimd.memset(sc_i32[64:P, :], 0)
-
-        nb_got = sb.tile([P, N], F32, name="nb_got", tag="bias_then_planes", align_bytes=64)
-        nc.vector.tensor_copy(nb_got[:], nb_win[:].indirect(offsets[:]))
         sc_got = sb.tile([P, N], U8, name="sc_got", align_bytes=64)
         nc.vector.tensor_copy(sc_got[:], sc_win[:].indirect(offsets[:]))
+
+        nc.vector.memset(nb_win[0:BIAS_ROW, 0:967], 0.0)
+        nc.vector.memset(nb_win[0:BIAS_ROW, 967:1936], 0.0)
+        nc.gpsimd.memset(nb_win[0:BIAS_ROW, 1936:T], 0.0)
+
+        planes = sb.tile([P, PASSES, N], U8, name="planes", align_bytes=64)
+        planes_i32 = planes[:].bitcast(I32)
+        sc_got_i32 = sc_got[:].bitcast(I32)
+        for quad in range(4):
+            nc.scalar.dma_start(planes_i32[32 * quad : 32 * quad + 4, :, :], sc_got_i32[8 * quad : 8 * quad + 8, :])
+
+        nb_got = shared.tile([P, N], F32, name="nb_got", offset=5120, align_bytes=64)
+        nc.vector.tensor_copy(nb_got[:], nb_win[:].indirect(offsets[:]))
 
         turned = ps.tile([P, NCH, CH], F32, name="turned")
         for c in range(NCH):
@@ -65,20 +76,14 @@ def tile_attend_neu_relu_topk_kernel(tc, qT, k_words, k_scales, nb, offs, out):
         nb_col = sb.tile([P, NCH], F32, name="nb_col")
         nc.scalar.copy(nb_col[:], turned[:, :, BIAS_ROW])
 
-        planes = sb.tile([P, PASSES, N], U8, name="planes", tag="bias_then_planes", align_bytes=64)
-        planes_i32 = planes[:].bitcast(I32)
-        sc_got_i32 = sc_got[:].bitcast(I32)
-        for quad in range(4):
-            nc.scalar.dma_start(planes_i32[32 * quad : 32 * quad + 4, :, :], sc_got_i32[8 * quad : 8 * quad + 8, :])
-
-        w_got = sb.tile([P, N], U32, name="w_got", align_bytes=64)
+        w_got = sb.tile([P, N], U32, name="w_got", tag="nb_win", align_bytes=64)
         nc.vector.tensor_copy(w_got[:], w_win[:].bitcast(U32).indirect(offsets[:]))
 
         spread = ps.tile([P, N], F32, name="spread")
         for c in range(NCH):
             nc.tensor.transpose(spread[:, c * CH : (c + 1) * CH], nb_col[:, c : c + 1].to_broadcast([P, P]), ident[:])
 
-        q_bf = [sb.tile([P, NQ, PACK], BF16, name="q_bf%d" % o, align_bytes=64) for o in range(PASSES)]
+        q_bf = [shared.tile([P, NQ, PACK], BF16, name="q_bf%d" % o, offset=5120 + 1024 * o, align_bytes=64) for o in range(PASSES)]
         q_codes = [sb.tile([P, NQ], U32, name="q_codes%d" % o, align_bytes=64) for o in range(PASSES)]
         q_scales = [sb.tile([P, NQ], U8, name="q_scales%d" % o, align_bytes=64) for o in range(PASSES)]
         for o in range(PASSES):
@@ -132,10 +137,13 @@ def tile_attend_neu_relu_topk_kernel(tc, qT, k_words, k_scales, nb, offs, out):
             cols = slice(c * CH, (c + 1) * CH)
             summed = sb.tile([P, CH], F32, name="summed%d" % c)
             nc.vector.tensor_tensor(summed[:], acc[c][:], bias[:, cols], ALU.add)
-            nc.scalar.activation(res[:, cols], summed[:], ACT.Relu)
+            if c < NCH - 1:
+                nc.scalar.activation(res[:, cols], summed[:], ACT.Relu)
+            else:
+                nc.vector.tensor_scalar_max(res[:, cols], summed[:], 0.0)
             if c == 1:
                 nc.sync.dma_start(out[0, :, 0 : 2 * CH], res[:, 0 : 2 * CH])
             if c == 2:
-                nc.sync.dma_start(out[0, :, cols], res[:, cols])
-            if c == 3:
                 nc.scalar.dma_start(out[0, :, cols], res[:, cols])
+            if c == 3:
+                nc.sync.dma_start(out[0, :, cols], res[:, cols])

@@ -40,7 +40,9 @@ def tile_attend_neu_relu_topk_kernel(tc, qT, k_words, k_scales, nb, offs, out):
         offsets = sb.tile([P, N // 16], U16, name="offsets")
         nc.sync.dma_start(offsets[:], offs)
         w_win = sb.tile([P, T], I32, name="w_win", align_bytes=64)
-        nc.sync.dma_start(w_win[:], k_words[0].rearrange("p t b -> p (t b)").bitcast(I32))
+        words = k_words[0].rearrange("p t b -> p (t b)").bitcast(I32)
+        nc.sync.dma_start(w_win[:, 0 : T // 2], words[:, 0 : T // 2])
+        nc.scalar.dma_start(w_win[:, T // 2 : T], words[:, T // 2 : T])
         q_raw = [shared.tile([P, PACK, NQ], F32, name="q_raw%d" % o, offset=2048 * o, align_bytes=64) for o in range(PASSES)]
         for o in range(PASSES):
             nc.sync.dma_start(q_raw[o][:], qT[0, 512 * o : 512 * (o + 1), :].rearrange("(p j) w -> p j w", j=PACK))
@@ -70,18 +72,20 @@ def tile_attend_neu_relu_topk_kernel(tc, qT, k_words, k_scales, nb, offs, out):
         nb_got = shared.tile([P, N], F32, name="nb_got", offset=5120, align_bytes=64)
         nc.vector.tensor_copy(nb_got[:], nb_win[:].indirect(offsets[:]))
 
-        turned = ps.tile([P, NCH, CH], F32, name="turned")
-        for c in range(NCH):
-            nc.tensor.transpose(turned[:, c, :], nb_got[:, c * CH : (c + 1) * CH], ident[:])
-        nb_col = sb.tile([P, NCH], F32, name="nb_col")
-        nc.scalar.copy(nb_col[:], turned[:, :, BIAS_ROW])
+        nb_col = [sb.tile([P, 2], F32, name="nb_col%d" % h) for h in range(2)]
+        for h in range(2):
+            turned = ps.tile([P, 2, CH], F32, name="turned%d" % h)
+            for i in range(2):
+                c = 2 * h + i
+                nc.tensor.transpose(turned[:, i, :], nb_got[:, c * CH : (c + 1) * CH], ident[:])
+            nc.scalar.copy(nb_col[h][:], turned[:, :, BIAS_ROW])
 
         w_got = sb.tile([P, N], U32, name="w_got", tag="nb_win", align_bytes=64)
         nc.vector.tensor_copy(w_got[:], w_win[:].bitcast(U32).indirect(offsets[:]))
 
         spread = ps.tile([P, N], F32, name="spread")
         for c in range(NCH):
-            nc.tensor.transpose(spread[:, c * CH : (c + 1) * CH], nb_col[:, c : c + 1].to_broadcast([P, P]), ident[:])
+            nc.tensor.transpose(spread[:, c * CH : (c + 1) * CH], nb_col[c // 2][:, c % 2 : c % 2 + 1].to_broadcast([P, P]), ident[:])
 
         q_bf = [shared.tile([P, NQ, PACK], BF16, name="q_bf%d" % o, offset=5120 + 1024 * o, align_bytes=64) for o in range(PASSES)]
         q_codes = [sb.tile([P, NQ], U32, name="q_codes%d" % o, align_bytes=64) for o in range(PASSES)]

@@ -23,6 +23,7 @@ PASSES = 2
 CH = 128
 NCH = N // CH
 BIAS_ROW = P - 1
+QH = NQ // 2
 
 
 def tile_attend_neu_relu_topk_kernel(tc, qT, k_words, k_scales, nb, offs, out):
@@ -91,23 +92,26 @@ def tile_attend_neu_relu_topk_kernel(tc, qT, k_words, k_scales, nb, offs, out):
         q_codes = [sb.tile([P, NQ], U32, name="q_codes%d" % o, align_bytes=64) for o in range(PASSES)]
         q_scales = [sb.tile([P, NQ], U8, name="q_scales%d" % o, align_bytes=64) for o in range(PASSES)]
         for o in range(PASSES):
-            nc.scalar.copy(
-                q_bf[o][:].rearrange("p (c i) t -> p c t i", i=4),
-                q_raw[o][:].rearrange("p t (c i) -> p c t i", i=4),
-            )
+            for h in range(2):
+                rows = slice(h * QH, (h + 1) * QH)
+                nc.scalar.copy(
+                    q_bf[o][:, rows, :].rearrange("p (c i) t -> p c t i", i=4),
+                    q_raw[o][:, :, rows].rearrange("p t (c i) -> p c t i", i=4),
+                )
 
         bias = shared.tile([P, N], F32, name="bias", offset=3072, align_bytes=64)
         for h in range(2):
             nc.scalar.copy(bias[:, h * 2 * CH : (h + 1) * 2 * CH], spread[:, h * 2 * CH : (h + 1) * 2 * CH])
 
-        def quantize(o):
+        def quantize(o, h):
+            rows = slice(h * QH, (h + 1) * QH)
             nc.vector.quantize_mx(
-                out=q_codes[o][:].bitcast(FP8X4),
-                scales=q_scales[o][:],
-                in_=q_bf[o][:].rearrange("p w j -> p (w j)"),
+                out=q_codes[o][:, rows].bitcast(FP8X4),
+                scales=q_scales[o][:, rows],
+                in_=q_bf[o][:, rows, :].rearrange("p w j -> p (w j)"),
             )
 
-        keys = [shared.tile([P, 2 * N], U8, name="keys%d" % o, offset=2048 * o, align_bytes=64) for o in range(PASSES)]
+        keys = [shared.tile([P, 2 * N], U8, name="keys%d" % o, offset=5120 * o, align_bytes=64) for o in range(PASSES)]
         halves = w_got[:].bitcast(U16).rearrange("p (c n h) -> p h c n", h=PASSES, c=NCH)
 
         def split(o, lo, hi):
@@ -126,11 +130,13 @@ def tile_attend_neu_relu_topk_kernel(tc, qT, k_words, k_scales, nb, offs, out):
                 stop=(o == PASSES - 1),
             )
 
-        quantize(0)
-        split(0, 0, 2)
-        split(0, 2, 4)
-        quantize(1)
+        quantize(0, 0)
+        quantize(0, 1)
+        split(0, 0, 1)
+        split(0, 1, 4)
         split(1, 0, 2)
+        quantize(1, 0)
+        quantize(1, 1)
         split(1, 2, 4)
         for o in range(PASSES):
             for c in range(NCH):
@@ -145,9 +151,5 @@ def tile_attend_neu_relu_topk_kernel(tc, qT, k_words, k_scales, nb, offs, out):
                 nc.scalar.activation(res[:, cols], summed[:], ACT.Relu)
             else:
                 nc.vector.tensor_scalar_max(res[:, cols], summed[:], 0.0)
-            if c == 1:
-                nc.sync.dma_start(out[0, :, 0 : 2 * CH], res[:, 0 : 2 * CH])
-            if c == 2:
-                nc.scalar.dma_start(out[0, :, cols], res[:, cols])
-            if c == 3:
-                nc.sync.dma_start(out[0, :, cols], res[:, cols])
+            queue = nc.scalar if c == NCH - 2 else nc.sync
+            queue.dma_start(out[0, :, cols], res[:, cols])

@@ -68,7 +68,8 @@ def tile_attend_neu_relu_topk_kernel(tc, qT, k_words, k_scales, nb, offs, out):
         planes_i32 = planes[:].bitcast(I32)
         sc_got_i32 = sc_got[:].bitcast(I32)
         for quad in range(4):
-            nc.scalar.dma_start(planes_i32[32 * quad : 32 * quad + 4, :, :], sc_got_i32[8 * quad : 8 * quad + 8, :])
+            queue = nc.sync if quad % 2 else nc.scalar
+            queue.dma_start(planes_i32[32 * quad : 32 * quad + 4, :, :], sc_got_i32[8 * quad : 8 * quad + 8, :])
 
         nb_got = shared.tile([P, N], F32, name="nb_got", offset=5120, align_bytes=64)
         nc.vector.tensor_copy(nb_got[:], nb_win[:].indirect(offsets[:]))

@@ -24,6 +24,7 @@ CH = 128
 NCH = N // CH
 BIAS_ROW = P - 1
 QH = NQ // 2
+SYNC_COLS = 2208
 
 
 def tile_attend_neu_relu_topk_kernel(tc, qT, k_words, k_scales, nb, offs, out):
@@ -42,8 +43,8 @@ def tile_attend_neu_relu_topk_kernel(tc, qT, k_words, k_scales, nb, offs, out):
         nc.sync.dma_start(offsets[:], offs)
         w_win = sb.tile([P, T], I32, name="w_win", align_bytes=64)
         words = k_words[0].rearrange("p t b -> p (t b)").bitcast(I32)
-        nc.sync.dma_start(w_win[:, 0 : T // 2], words[:, 0 : T // 2])
-        nc.scalar.dma_start(w_win[:, T // 2 : T], words[:, T // 2 : T])
+        nc.sync.dma_start(w_win[:, 0:SYNC_COLS], words[:, 0:SYNC_COLS])
+        nc.scalar.dma_start(w_win[:, SYNC_COLS:T], words[:, SYNC_COLS:T])
         q_raw = [shared.tile([P, PACK, NQ], F32, name="q_raw%d" % o, offset=2048 * o, align_bytes=64) for o in range(PASSES)]
         for o in range(PASSES):
             nc.sync.dma_start(q_raw[o][:], qT[0, 512 * o : 512 * (o + 1), :].rearrange("(p j) w -> p j w", j=PACK))

@@ -24,7 +24,7 @@ CH = 128
 NCH = N // CH
 BIAS_ROW = P - 1
 QH = NQ // 2
-SYNC_COLS = 2208
+SYNC_COLS = 3072
 
 
 def tile_attend_neu_relu_topk_kernel(tc, qT, k_words, k_scales, nb, offs, out):
@@ -69,8 +69,7 @@ def tile_attend_neu_relu_topk_kernel(tc, qT, k_words, k_scales, nb, offs, out):
         planes_i32 = planes[:].bitcast(I32)
         sc_got_i32 = sc_got[:].bitcast(I32)
         for quad in range(4):
-            queue = nc.sync if quad % 2 else nc.scalar
-            queue.dma_start(planes_i32[32 * quad : 32 * quad + 4, :, :], sc_got_i32[8 * quad : 8 * quad + 8, :])
+            nc.scalar.dma_start(planes_i32[32 * quad : 32 * quad + 4, :, :], sc_got_i32[8 * quad : 8 * quad + 8, :])
 
         nb_got = shared.tile([P, N], F32, name="nb_got", offset=5120, align_bytes=64)
         nc.vector.tensor_copy(nb_got[:], nb_win[:].indirect(offsets[:]))

@@ -69,7 +69,8 @@ def tile_attend_neu_relu_topk_kernel(tc, qT, k_words, k_scales, nb, offs, out):
         planes_i32 = planes[:].bitcast(I32)
         sc_got_i32 = sc_got[:].bitcast(I32)
         for quad in range(4):
-            nc.scalar.dma_start(planes_i32[32 * quad : 32 * quad + 4, :, :], sc_got_i32[8 * quad : 8 * quad + 8, :])
+            queue = nc.scalar if quad >= 2 else nc.sync
+            queue.dma_start(planes_i32[32 * quad : 32 * quad + 4, :, :], sc_got_i32[8 * quad : 8 * quad + 8, :])
 
         nb_got = shared.tile([P, N], F32, name="nb_got", offset=5120, align_bytes=64)
         nc.vector.tensor_copy(nb_got[:], nb_win[:].indirect(offsets[:]))

@@ -73,7 +73,8 @@ def tile_attend_neu_relu_topk_kernel(tc, qT, k_words, k_scales, nb, offs, out):
             queue.dma_start(planes_i32[32 * quad : 32 * quad + 4, :, :], sc_got_i32[8 * quad : 8 * quad + 8, :])
 
         nb_got = shared.tile([P, N], F32, name="nb_got", offset=5120, align_bytes=64)
-        nc.vector.tensor_copy(nb_got[:], nb_win[:].indirect(offsets[:]))
+        nc.vector.tensor_copy(nb_got[:, 0 : N // 2], nb_win[:].indirect(offsets[:, 0 : N // 32]))
+        nc.scalar.activation(nb_got[:, N // 2 : N], nb_win[:].indirect(offsets[:, N // 32 : N // 16]), ACT.Copy)
 
         nb_col = [sb.tile([P, 2], F32, name="nb_col%d" % h) for h in range(2)]
         for h in range(2):

@@ -91,34 +91,37 @@ def tile_attend_neu_relu_topk_kernel(tc, qT, k_words, k_scales, nb, offs, out):
         for c in range(NCH):
             nc.tensor.transpose(spread[:, c * CH : (c + 1) * CH], nb_col[c // 2][:, c % 2 : c % 2 + 1].to_broadcast([P, P]), ident[:])
 
-        q_bf = [shared.tile([P, NQ, PACK], BF16, name="q_bf%d" % o, offset=5120 + 1024 * o, align_bytes=64) for o in range(PASSES)]
+        q_bf0 = shared.tile([P, NQ, PACK], BF16, name="q_bf0", offset=5120, align_bytes=64)
+        q_bf1 = shared.tile([P, NQ, PACK], BF16, name="q_bf1", offset=6144, align_bytes=64)
         q_codes = [sb.tile([P, NQ], U32, name="q_codes%d" % o, align_bytes=64) for o in range(PASSES)]
         q_scales = [sb.tile([P, NQ], U8, name="q_scales%d" % o, align_bytes=64) for o in range(PASSES)]
-        for o in range(PASSES):
-            for h in range(2):
-                rows = slice(h * QH, (h + 1) * QH)
-                nc.scalar.copy(
-                    q_bf[o][:, rows, :].rearrange("p (c i) t -> p c t i", i=4),
-                    q_raw[o][:, :, rows].rearrange("p t (c i) -> p c t i", i=4),
-                )
+        halves = [slice(0, QH), slice(QH, NQ)]
+
+        def cast(copy, grouped, raw):
+            copy(grouped.rearrange("p (c i) t -> p c t i", i=4), raw.rearrange("p t (c i) -> p c t i", i=4))
+
+        cast(nc.vector.tensor_copy, q_bf1[:, halves[1], :], q_raw[1][:, :, halves[1]])
+        cast(nc.scalar.copy, q_bf0[:], q_raw[0][:])
+        cast(nc.scalar.copy, q_bf1[:, halves[0], :], q_raw[1][:, :, halves[0]])
 
         bias = shared.tile([P, N], F32, name="bias", offset=3072, align_bytes=64)
         for h in range(2):
             nc.scalar.copy(bias[:, h * 2 * CH : (h + 1) * 2 * CH], spread[:, h * 2 * CH : (h + 1) * 2 * CH])
 
-        def quantize(o, h):
-            rows = slice(h * QH, (h + 1) * QH)
+        def quantize(o, rows, grouped):
             nc.vector.quantize_mx(
                 out=q_codes[o][:, rows].bitcast(FP8X4),
                 scales=q_scales[o][:, rows],
-                in_=q_bf[o][:, rows, :].rearrange("p w j -> p (w j)"),
+                in_=grouped.rearrange("p w j -> p (w j)"),
             )
 
-        keys = [shared.tile([P, 2 * N], U8, name="keys%d" % o, offset=5120 * o, align_bytes=64) for o in range(PASSES)]
-        halves = w_got[:].bitcast(U16).rearrange("p (c n h) -> p h c n", h=PASSES, c=NCH)
+        first_keys = shared.tile([P, 4 * CH], U8, name="first_keys", offset=0, align_bytes=64)
+        other_keys = shared.tile([P, 12 * CH], U8, name="other_keys", offset=1536, align_bytes=64)
+        keys = [first_keys[:]] + [other_keys[:, 4 * CH * c : 4 * CH * (c + 1)] for c in range(NCH - 1)]
+        pairs = w_got[:].bitcast(U16).rearrange("p (c n o) -> p c o n", o=PASSES, c=NCH)
 
-        def split(o, lo, hi):
-            nc.vector.tensor_copy(keys[o][:].bitcast(U16).rearrange("p (c n) -> p c n", c=NCH)[:, lo:hi, :], halves[:, o, lo:hi, :])
+        def split(c):
+            nc.vector.tensor_copy(keys[c].bitcast(U16).rearrange("p (o n) -> p o n", o=PASSES), pairs[:, c, :, :])
 
         acc = [ps.tile([P, CH], F32, name="acc%d" % c) for c in range(NCH)]
 
@@ -127,22 +130,19 @@ def tile_attend_neu_relu_topk_kernel(tc, qT, k_words, k_scales, nb, offs, out):
                 out=acc[c][:],
                 lhsT=q_codes[o][:].bitcast(FP8X4),
                 lhsT_scale=q_scales[o][:],
-                rhs=keys[o][:, 2 * c * CH : 2 * (c + 1) * CH].bitcast(FP4X4),
+                rhs=keys[c][:, 2 * CH * o : 2 * CH * (o + 1)].bitcast(FP4X4),
                 rhs_scale=planes[:, o, c * CH : (c + 1) * CH],
                 start=(o == 0),
                 stop=(o == PASSES - 1),
             )
 
-        quantize(0, 0)
-        quantize(0, 1)
-        split(0, 0, 1)
-        split(0, 1, 4)
-        split(1, 0, 2)
-        quantize(1, 0)
-        quantize(1, 1)
-        split(1, 2, 4)
-        for o in range(PASSES):
-            for c in range(NCH):
+        quantize(0, slice(0, NQ), q_bf0[:])
+        split(0)
+        quantize(1, slice(0, NQ), q_bf1[:])
+        for c in range(1, NCH):
+            split(c)
+        for c in range(NCH):
+            for o in range(PASSES):
                 multiply(c, o)
 
         res = sb.tile([P, N], F32, name="res")

@@ -22,9 +22,12 @@ PACK = 4
 PASSES = 2
 CH = 128
 NCH = N // CH
-BIAS_ROW = P - 1
+ROW_LOW = P - 1
+ROW_HIGH = P - 5
+ROW_STEP = 3
+HALF = T // 2
 QH = NQ // 2
-SYNC_COLS = 3072
+FIRST_COLS = 1856
 
 
 def tile_attend_neu_relu_topk_kernel(tc, qT, k_words, k_scales, nb, offs, out):
@@ -34,62 +37,69 @@ def tile_attend_neu_relu_topk_kernel(tc, qT, k_words, k_scales, nb, offs, out):
         shared = ctx.enter_context(tc.tile_pool(name="shared", bufs=1))
         ps = ctx.enter_context(tc.psum_pool(name="ps", bufs=1))
 
-        sc_win = sb.tile([P, T], U8, name="sc_win", align_bytes=64)
-        sc_i32 = sc_win[:].bitcast(I32)
-        nc.sync.dma_start(sc_i32[0:32, :], k_scales.rearrange("o f t -> f o t").bitcast(I32))
-        nb_win = sb.tile([P, T], F32, name="nb_win", align_bytes=64)
-        nc.scalar.dma_start(nb_win[BIAS_ROW:P, :], nb[0:1, :])
         offsets = sb.tile([P, N // 16], U16, name="offsets")
         nc.sync.dma_start(offsets[:], offs)
+        nb_win = sb.tile([P, T], F32, name="nb_win", align_bytes=64)
+        nc.sync.dma_start(nb_win[ROW_LOW : ROW_LOW + 1, 0:HALF], nb[0:1, 0:HALF])
         w_win = sb.tile([P, T], I32, name="w_win", align_bytes=64)
         words = k_words[0].rearrange("p t b -> p (t b)").bitcast(I32)
-        nc.sync.dma_start(w_win[:, 0:SYNC_COLS], words[:, 0:SYNC_COLS])
-        nc.scalar.dma_start(w_win[:, SYNC_COLS:T], words[:, SYNC_COLS:T])
+        nc.scalar.dma_start(w_win[:, 0:FIRST_COLS], words[:, 0:FIRST_COLS])
+
+        sc_win = sb.tile([P, T], U8, name="sc_win", align_bytes=64)
+        sc_i32 = sc_win[:].bitcast(I32)
+        nc.vector.memset(sc_i32[:, 0:255], 0)
+        nc.vector.memset(sc_i32[:, 255:512], 0)
+        nc.gpsimd.memset(sc_i32[:, 512:1024], 0)
+        nc.scalar.dma_start(sc_i32[0 : 32 * ROW_STEP : ROW_STEP, :], k_scales.rearrange("o f t -> f o t").bitcast(I32))
+
+        nc.vector.memset(nb_win[:, HALF : HALF + 447], 0.0)
+        nc.vector.memset(nb_win[:, HALF + 447 : HALF + 896], 0.0)
+        nc.gpsimd.memset(nb_win[:, HALF + 896 : T], 0.0)
+        nc.sync.dma_start(nb_win[ROW_HIGH : ROW_HIGH + 1, HALF:T], nb[0:1, HALF:T])
+        nc.sync.dma_start(w_win[:, FIRST_COLS:T], words[:, FIRST_COLS:T])
         q_raw = [shared.tile([P, PACK, NQ], F32, name="q_raw%d" % o, offset=2048 * o, align_bytes=64) for o in range(PASSES)]
         for o in range(PASSES):
             nc.sync.dma_start(q_raw[o][:], qT[0, 512 * o : 512 * (o + 1), :].rearrange("(p j) w -> p j w", j=PACK))
 
-        ident = sb.tile([P, P], F32, name="ident")
+        nc.vector.memset(nb_win[0:ROW_LOW, 0:511], 0.0)
+        nc.vector.memset(nb_win[0:ROW_LOW, 511:1024], 0.0)
         ramp = sb.tile([P, P], F32, name="ramp")
         nc.gpsimd.iota(ramp[:], [[1, P]], base=0, channel_multiplier=-1, allow_small_or_imprecise_dtypes=True)
+        nc.gpsimd.memset(nb_win[0:ROW_LOW, 1024:HALF], 0.0)
+        ident = sb.tile([P, P], F32, name="ident")
         dist = sb.tile([P, P], F32, name="dist")
         nc.scalar.activation(dist[:], ramp[:], ACT.Abs)
         nc.scalar.activation(ident[:], dist[:], ACT.Relu, bias=1.0, scale=-1.0)
-        nc.vector.memset(sc_i32[32:64, 0:511], 0)
-        nc.vector.memset(sc_i32[32:64, 511:1024], 0)
-        nc.gpsimd.memset(sc_i32[64:P, :], 0)
+
         sc_got = sb.tile([P, N], U8, name="sc_got", align_bytes=64)
         nc.vector.tensor_copy(sc_got[:], sc_win[:].indirect(offsets[:]))
-
-        nc.vector.memset(nb_win[0:BIAS_ROW, 0:967], 0.0)
-        nc.vector.memset(nb_win[0:BIAS_ROW, 967:1936], 0.0)
-        nc.gpsimd.memset(nb_win[0:BIAS_ROW, 1936:T], 0.0)
-
         planes = sb.tile([P, PASSES, N], U8, name="planes", align_bytes=64)
         planes_i32 = planes[:].bitcast(I32)
         sc_got_i32 = sc_got[:].bitcast(I32)
         for quad in range(4):
-            queue = nc.scalar if quad >= 2 else nc.sync
-            queue.dma_start(planes_i32[32 * quad : 32 * quad + 4, :, :], sc_got_i32[8 * quad : 8 * quad + 8, :])
+            rows = slice(8 * ROW_STEP * quad, 8 * ROW_STEP * (quad + 1), ROW_STEP)
+            nc.sync.dma_start(planes_i32[32 * quad : 32 * quad + 4, :, :], sc_got_i32[rows, :])
 
         nb_got = shared.tile([P, N], F32, name="nb_got", offset=5120, align_bytes=64)
-        nc.vector.tensor_copy(nb_got[:, 0 : N // 2], nb_win[:].indirect(offsets[:, 0 : N // 32]))
-        nc.scalar.activation(nb_got[:, N // 2 : N], nb_win[:].indirect(offsets[:, N // 32 : N // 16]), ACT.Copy)
+        nc.scalar.activation(nb_got[:, 0 : N // 2], nb_win[:].indirect(offsets[:, 0 : N // 32]), ACT.Copy)
+        nc.vector.tensor_copy(nb_got[:, N // 2 : N], nb_win[:].indirect(offsets[:, N // 32 : N // 16]))
 
-        nb_col = [sb.tile([P, 2], F32, name="nb_col%d" % h) for h in range(2)]
+        nb_col = [sb.tile([P, 2, 2], F32, name="nb_col%d" % h) for h in range(2)]
         for h in range(2):
             turned = ps.tile([P, 2, CH], F32, name="turned%d" % h)
             for i in range(2):
                 c = 2 * h + i
                 nc.tensor.transpose(turned[:, i, :], nb_got[:, c * CH : (c + 1) * CH], ident[:])
-            nc.scalar.copy(nb_col[h][:], turned[:, :, BIAS_ROW])
+            nc.scalar.copy(nb_col[h][:], turned[:, :, ROW_HIGH : ROW_LOW + 1 : ROW_LOW - ROW_HIGH])
 
         w_got = sb.tile([P, N], U32, name="w_got", tag="nb_win", align_bytes=64)
         nc.vector.tensor_copy(w_got[:], w_win[:].bitcast(U32).indirect(offsets[:]))
 
         spread = ps.tile([P, N], F32, name="spread")
         for c in range(NCH):
-            nc.tensor.transpose(spread[:, c * CH : (c + 1) * CH], nb_col[c // 2][:, c % 2 : c % 2 + 1].to_broadcast([P, P]), ident[:])
+            for r in range(2):
+                column = nb_col[c // 2][:, c % 2, r : r + 1].to_broadcast([P, P])
+                nc.tensor.matmul(spread[:, c * CH : (c + 1) * CH], column, ident[:], start=(r == 0), stop=(r == 1), is_transpose=True)
 
         q_bf0 = shared.tile([P, NQ, PACK], BF16, name="q_bf0", offset=5120, align_bytes=64)
         q_bf1 = shared.tile([P, NQ, PACK], BF16, name="q_bf1", offset=6144, align_bytes=64)

@@ -27,7 +27,8 @@ ROW_HIGH = P - 5
 ROW_STEP = 3
 HALF = T // 2
 QH = NQ // 2
-FIRST_COLS = 1856
+FIRST_COLS = 640
+SECOND_END = 1664
 
 
 def tile_attend_neu_relu_topk_kernel(tc, qT, k_words, k_scales, nb, offs, out):
@@ -51,21 +52,22 @@ def tile_attend_neu_relu_topk_kernel(tc, qT, k_words, k_scales, nb, offs, out):
         nc.vector.memset(sc_i32[:, 255:512], 0)
         nc.gpsimd.memset(sc_i32[:, 512:1024], 0)
         nc.scalar.dma_start(sc_i32[0 : 32 * ROW_STEP : ROW_STEP, :], k_scales.rearrange("o f t -> f o t").bitcast(I32))
+        nc.scalar.dma_start(w_win[:, FIRST_COLS:SECOND_END], words[:, FIRST_COLS:SECOND_END])
 
         nc.vector.memset(nb_win[:, HALF : HALF + 447], 0.0)
         nc.vector.memset(nb_win[:, HALF + 447 : HALF + 896], 0.0)
         nc.gpsimd.memset(nb_win[:, HALF + 896 : T], 0.0)
         nc.sync.dma_start(nb_win[ROW_HIGH : ROW_HIGH + 1, HALF:T], nb[0:1, HALF:T])
-        nc.sync.dma_start(w_win[:, FIRST_COLS:T], words[:, FIRST_COLS:T])
+        nc.sync.dma_start(w_win[:, SECOND_END:T], words[:, SECOND_END:T])
         q_raw = [shared.tile([P, PACK, NQ], F32, name="q_raw%d" % o, offset=2048 * o, align_bytes=64) for o in range(PASSES)]
         for o in range(PASSES):
             nc.sync.dma_start(q_raw[o][:], qT[0, 512 * o : 512 * (o + 1), :].rearrange("(p j) w -> p j w", j=PACK))
 
-        nc.vector.memset(nb_win[0:ROW_LOW, 0:511], 0.0)
-        nc.vector.memset(nb_win[0:ROW_LOW, 511:1024], 0.0)
+        nc.vector.memset(nb_win[0:ROW_LOW, 0:255], 0.0)
+        nc.vector.memset(nb_win[0:ROW_LOW, 255:512], 0.0)
         ramp = sb.tile([P, P], F32, name="ramp")
         nc.gpsimd.iota(ramp[:], [[1, P]], base=0, channel_multiplier=-1, allow_small_or_imprecise_dtypes=True)
-        nc.gpsimd.memset(nb_win[0:ROW_LOW, 1024:HALF], 0.0)
+        nc.gpsimd.memset(nb_win[0:ROW_LOW, 512:HALF], 0.0)
         ident = sb.tile([P, P], F32, name="ident")
         dist = sb.tile([P, P], F32, name="dist")
         nc.scalar.activation(dist[:], ramp[:], ACT.Abs)
@@ -81,25 +83,26 @@ def tile_attend_neu_relu_topk_kernel(tc, qT, k_words, k_scales, nb, offs, out):
             nc.sync.dma_start(planes_i32[32 * quad : 32 * quad + 4, :, :], sc_got_i32[rows, :])
 
         nb_got = shared.tile([P, N], F32, name="nb_got", offset=5120, align_bytes=64)
-        nc.scalar.activation(nb_got[:, 0 : N // 2], nb_win[:].indirect(offsets[:, 0 : N // 32]), ACT.Copy)
-        nc.vector.tensor_copy(nb_got[:, N // 2 : N], nb_win[:].indirect(offsets[:, N // 32 : N // 16]))
+        nc.vector.tensor_copy(nb_got[:, 0 : N // 2], nb_win[:].indirect(offsets[:, 0 : N // 32]))
+        nc.scalar.activation(nb_got[:, N // 2 : N], nb_win[:].indirect(offsets[:, N // 32 : N // 16]), ACT.Copy)
 
-        nb_col = [sb.tile([P, 2, 2], F32, name="nb_col%d" % h) for h in range(2)]
+        nb_low = [sb.tile([P, 2], F32, name="nb_low%d" % h) for h in range(2)]
+        nb_col = [sb.tile([P, 1], F32, name="nb_col%d" % c) for c in range(NCH)]
         for h in range(2):
             turned = ps.tile([P, 2, CH], F32, name="turned%d" % h)
             for i in range(2):
                 c = 2 * h + i
                 nc.tensor.transpose(turned[:, i, :], nb_got[:, c * CH : (c + 1) * CH], ident[:])
-            nc.scalar.copy(nb_col[h][:], turned[:, :, ROW_HIGH : ROW_LOW + 1 : ROW_LOW - ROW_HIGH])
+            nc.scalar.copy(nb_low[h][:], turned[:, :, ROW_LOW])
+            for i in range(2):
+                nc.scalar.activation(nb_col[2 * h + i][:], turned[:, i, ROW_HIGH : ROW_HIGH + 1], ACT.Identity, bias=nb_low[h][:, i : i + 1])
 
         w_got = sb.tile([P, N], U32, name="w_got", tag="nb_win", align_bytes=64)
         nc.vector.tensor_copy(w_got[:], w_win[:].bitcast(U32).indirect(offsets[:]))
 
         spread = ps.tile([P, N], F32, name="spread")
         for c in range(NCH):
-            for r in range(2):
-                column = nb_col[c // 2][:, c % 2, r : r + 1].to_broadcast([P, P])
-                nc.tensor.matmul(spread[:, c * CH : (c + 1) * CH], column, ident[:], start=(r == 0), stop=(r == 1), is_transpose=True)
+            nc.tensor.transpose(spread[:, c * CH : (c + 1) * CH], nb_col[c][:].to_broadcast([P, P]), ident[:])
 
         q_bf0 = shared.tile([P, NQ, PACK], BF16, name="q_bf0", offset=5120, align_bytes=64)
         q_bf1 = shared.tile([P, NQ, PACK], BF16, name="q_bf1", offset=6144, align_bytes=64)

@@ -28,7 +28,7 @@ ROW_STEP = 3
 HALF = T // 2
 QH = NQ // 2
 FIRST_COLS = 640
-SECOND_END = 1664
+SECOND_END = 2368
 
 
 def tile_attend_neu_relu_topk_kernel(tc, qT, k_words, k_scales, nb, offs, out):

@@ -27,7 +27,7 @@ ROW_HIGH = P - 5
 ROW_STEP = 3
 HALF = T // 2
 QH = NQ // 2
-FIRST_COLS = 640
+FIRST_COLS = 1344
 SECOND_END = 2368
 
 

@@ -27,8 +27,7 @@ ROW_HIGH = P - 5
 ROW_STEP = 3
 HALF = T // 2
 QH = NQ // 2
-FIRST_COLS = 1344
-SECOND_END = 2368
+FIRST_COLS = 2176
 
 
 def tile_attend_neu_relu_topk_kernel(tc, qT, k_words, k_scales, nb, offs, out):
@@ -46,32 +45,29 @@ def tile_attend_neu_relu_topk_kernel(tc, qT, k_words, k_scales, nb, offs, out):
         words = k_words[0].rearrange("p t b -> p (t b)").bitcast(I32)
         nc.scalar.dma_start(w_win[:, 0:FIRST_COLS], words[:, 0:FIRST_COLS])
 
+        ramp = sb.tile([P, P], F32, name="ramp")
+        nc.gpsimd.iota(ramp[:], [[1, P]], base=0, channel_multiplier=-1, allow_small_or_imprecise_dtypes=True)
+        ident = sb.tile([P, P], F32, name="ident")
+        dist = shared.tile([P, P], F32, name="dist", offset=6144, align_bytes=64)
+        nc.scalar.activation(dist[:], ramp[:], ACT.Abs)
+        nc.scalar.activation(ident[:], dist[:], ACT.Relu, bias=1.0, scale=-1.0)
+
+        nc.vector.memset(nb_win[:, HALF:T], 0.0)
+        nc.sync.dma_start(nb_win[ROW_HIGH : ROW_HIGH + 1, HALF:T], nb[0:1, HALF:T])
         sc_win = sb.tile([P, T], U8, name="sc_win", align_bytes=64)
         sc_i32 = sc_win[:].bitcast(I32)
-        nc.vector.memset(sc_i32[:, 0:255], 0)
-        nc.vector.memset(sc_i32[:, 255:512], 0)
-        nc.gpsimd.memset(sc_i32[:, 512:1024], 0)
-        nc.scalar.dma_start(sc_i32[0 : 32 * ROW_STEP : ROW_STEP, :], k_scales.rearrange("o f t -> f o t").bitcast(I32))
-        nc.scalar.dma_start(w_win[:, FIRST_COLS:SECOND_END], words[:, FIRST_COLS:SECOND_END])
-
-        nc.vector.memset(nb_win[:, HALF : HALF + 447], 0.0)
-        nc.vector.memset(nb_win[:, HALF + 447 : HALF + 896], 0.0)
-        nc.gpsimd.memset(nb_win[:, HALF + 896 : T], 0.0)
-        nc.sync.dma_start(nb_win[ROW_HIGH : ROW_HIGH + 1, HALF:T], nb[0:1, HALF:T])
-        nc.sync.dma_start(w_win[:, SECOND_END:T], words[:, SECOND_END:T])
+        nc.vector.memset(sc_i32[:], 0)
+        nc.sync.dma_start(sc_i32[0 : 32 * ROW_STEP : ROW_STEP, :], k_scales.rearrange("o f t -> f o t").bitcast(I32))
+        nc.sync.dma_start(w_win[:, FIRST_COLS:T], words[:, FIRST_COLS:T])
         q_raw = [shared.tile([P, PACK, NQ], F32, name="q_raw%d" % o, offset=2048 * o, align_bytes=64) for o in range(PASSES)]
         for o in range(PASSES):
             nc.sync.dma_start(q_raw[o][:], qT[0, 512 * o : 512 * (o + 1), :].rearrange("(p j) w -> p j w", j=PACK))
 
-        nc.vector.memset(nb_win[0:ROW_LOW, 0:255], 0.0)
-        nc.vector.memset(nb_win[0:ROW_LOW, 255:512], 0.0)
-        ramp = sb.tile([P, P], F32, name="ramp")
-        nc.gpsimd.iota(ramp[:], [[1, P]], base=0, channel_multiplier=-1, allow_small_or_imprecise_dtypes=True)
-        nc.gpsimd.memset(nb_win[0:ROW_LOW, 512:HALF], 0.0)
-        ident = sb.tile([P, P], F32, name="ident")
-        dist = sb.tile([P, P], F32, name="dist")
-        nc.scalar.activation(dist[:], ramp[:], ACT.Abs)
-        nc.scalar.activation(ident[:], dist[:], ACT.Relu, bias=1.0, scale=-1.0)
+        nc.vector.memset(nb_win[0:ROW_LOW, 0:HALF], 0.0)
+
+        nb_got = [shared.tile([P, N // 2], F32, name="nb_got%d" % h, offset=5120 + 1024 * h, align_bytes=64) for h in range(2)]
+        nc.vector.tensor_copy(nb_got[0][:], nb_win[:].indirect(offsets[:, 0 : N // 32]))
+        nc.scalar.activation(nb_got[1][:], nb_win[:].indirect(offsets[:, N // 32 : N // 16]), ACT.Copy)
 
         sc_got = sb.tile([P, N], U8, name="sc_got", align_bytes=64)
         nc.vector.tensor_copy(sc_got[:], sc_win[:].indirect(offsets[:]))
@@ -82,17 +78,12 @@ def tile_attend_neu_relu_topk_kernel(tc, qT, k_words, k_scales, nb, offs, out):
             rows = slice(8 * ROW_STEP * quad, 8 * ROW_STEP * (quad + 1), ROW_STEP)
             nc.sync.dma_start(planes_i32[32 * quad : 32 * quad + 4, :, :], sc_got_i32[rows, :])
 
-        nb_got = shared.tile([P, N], F32, name="nb_got", offset=5120, align_bytes=64)
-        nc.vector.tensor_copy(nb_got[:, 0 : N // 2], nb_win[:].indirect(offsets[:, 0 : N // 32]))
-        nc.scalar.activation(nb_got[:, N // 2 : N], nb_win[:].indirect(offsets[:, N // 32 : N // 16]), ACT.Copy)
-
         nb_low = [sb.tile([P, 2], F32, name="nb_low%d" % h) for h in range(2)]
         nb_col = [sb.tile([P, 1], F32, name="nb_col%d" % c) for c in range(NCH)]
         for h in range(2):
             turned = ps.tile([P, 2, CH], F32, name="turned%d" % h)
             for i in range(2):
-                c = 2 * h + i
-                nc.tensor.transpose(turned[:, i, :], nb_got[:, c * CH : (c + 1) * CH], ident[:])
+                nc.tensor.transpose(turned[:, i, :], nb_got[h][:, i * CH : (i + 1) * CH], ident[:])
             nc.scalar.copy(nb_low[h][:], turned[:, :, ROW_LOW])
             for i in range(2):
                 nc.scalar.activation(nb_col[2 * h + i][:], turned[:, i, ROW_HIGH : ROW_HIGH + 1], ACT.Identity, bias=nb_low[h][:, i : i + 1])
@@ -104,8 +95,8 @@ def tile_attend_neu_relu_topk_kernel(tc, qT, k_words, k_scales, nb, offs, out):
         for c in range(NCH):
             nc.tensor.transpose(spread[:, c * CH : (c + 1) * CH], nb_col[c][:].to_broadcast([P, P]), ident[:])
 
-        q_bf0 = shared.tile([P, NQ, PACK], BF16, name="q_bf0", offset=5120, align_bytes=64)
-        q_bf1 = shared.tile([P, NQ, PACK], BF16, name="q_bf1", offset=6144, align_bytes=64)
+        q_bf0 = shared.tile([P, NQ, PACK], BF16, name="q_bf0", offset=5632, align_bytes=64)
+        q_bf1 = shared.tile([P, NQ, PACK], BF16, name="q_bf1", offset=6656, align_bytes=64)
         q_codes = [sb.tile([P, NQ], U32, name="q_codes%d" % o, align_bytes=64) for o in range(PASSES)]
         q_scales = [sb.tile([P, NQ], U8, name="q_scales%d" % o, align_bytes=64) for o in range(PASSES)]
         halves = [slice(0, QH), slice(QH, NQ)]

@@ -26,7 +26,8 @@ ROW_LOW = P - 1
 ROW_HIGH = P - 5
 ROW_STEP = 3
 HALF = T // 2
-QH = NQ // 2
+SCALAR_ROWS = 96
+GP_START = 96
 FIRST_COLS = 2176
 
 
@@ -99,18 +100,17 @@ def tile_attend_neu_relu_topk_kernel(tc, qT, k_words, k_scales, nb, offs, out):
         q_bf1 = shared.tile([P, NQ, PACK], BF16, name="q_bf1", offset=6656, align_bytes=64)
         q_codes = [sb.tile([P, NQ], U32, name="q_codes%d" % o, align_bytes=64) for o in range(PASSES)]
         q_scales = [sb.tile([P, NQ], U8, name="q_scales%d" % o, align_bytes=64) for o in range(PASSES)]
-        halves = [slice(0, QH), slice(QH, NQ)]
+        halves = [slice(0, SCALAR_ROWS), slice(SCALAR_ROWS, NQ)]
 
         def cast(copy, grouped, raw):
             copy(grouped.rearrange("p (c i) t -> p c t i", i=4), raw.rearrange("p t (c i) -> p c t i", i=4))
 
-        cast(nc.vector.tensor_copy, q_bf1[:, halves[1], :], q_raw[1][:, :, halves[1]])
-        cast(nc.scalar.copy, q_bf0[:], q_raw[0][:])
-        cast(nc.scalar.copy, q_bf1[:, halves[0], :], q_raw[1][:, :, halves[0]])
+        def round_on_gpsimd(grouped, raw):
+            nc.gpsimd.tensor_scalar(grouped, raw, 1.0, 0.0, ALU.mult, ALU.add)
 
-        bias = shared.tile([P, N], F32, name="bias", offset=3072, align_bytes=64)
-        for h in range(2):
-            nc.scalar.copy(bias[:, h * 2 * CH : (h + 1) * 2 * CH], spread[:, h * 2 * CH : (h + 1) * 2 * CH])
+        cast(nc.scalar.copy, q_bf0[:, 0:GP_START, :], q_raw[0][:, :, 0:GP_START])
+        round_on_gpsimd(q_bf0[:, GP_START:NQ, :], q_raw[0][:, :, GP_START:NQ].rearrange("p t w -> p w t"))
+        cast(nc.scalar.copy, q_bf1[:, halves[0], :], q_raw[1][:, :, halves[0]])
 
         def quantize(o, rows, grouped):
             nc.vector.quantize_mx(
@@ -119,13 +119,18 @@ def tile_attend_neu_relu_topk_kernel(tc, qT, k_words, k_scales, nb, offs, out):
                 in_=grouped.rearrange("p w j -> p (w j)"),
             )
 
-        first_keys = shared.tile([P, 4 * CH], U8, name="first_keys", offset=0, align_bytes=64)
-        other_keys = shared.tile([P, 12 * CH], U8, name="other_keys", offset=1536, align_bytes=64)
-        keys = [first_keys[:]] + [other_keys[:, 4 * CH * c : 4 * CH * (c + 1)] for c in range(NCH - 1)]
+        early = [(0, 0), (1, 0), (0, 1), (2, 0)]
+        late = [(1, 1), (2, 1), (3, 0), (3, 1)]
+        early_keys = shared.tile([P, 4, 2 * CH], U8, name="early_keys", offset=1024, align_bytes=64)
+        late_keys = shared.tile([P, 4, 2 * CH], U8, name="late_keys", offset=2048, align_bytes=64)
+        keys = {}
+        for i in range(4):
+            keys[early[i]] = early_keys[:, i, :]
+            keys[late[i]] = late_keys[:, i, :]
         pairs = w_got[:].bitcast(U16).rearrange("p (c n o) -> p c o n", o=PASSES, c=NCH)
 
-        def split(c):
-            nc.vector.tensor_copy(keys[c].bitcast(U16).rearrange("p (o n) -> p o n", o=PASSES), pairs[:, c, :, :])
+        def split(c, o):
+            nc.vector.tensor_copy(keys[(c, o)].bitcast(U16), pairs[:, c, o, :])
 
         acc = [ps.tile([P, CH], F32, name="acc%d" % c) for c in range(NCH)]
 
@@ -134,20 +139,26 @@ def tile_attend_neu_relu_topk_kernel(tc, qT, k_words, k_scales, nb, offs, out):
                 out=acc[c][:],
                 lhsT=q_codes[o][:].bitcast(FP8X4),
                 lhsT_scale=q_scales[o][:],
-                rhs=keys[c][:, 2 * CH * o : 2 * CH * (o + 1)].bitcast(FP4X4),
+                rhs=keys[(c, o)].bitcast(FP4X4),
                 rhs_scale=planes[:, o, c * CH : (c + 1) * CH],
                 start=(o == 0),
                 stop=(o == PASSES - 1),
             )
 
         quantize(0, slice(0, NQ), q_bf0[:])
-        split(0)
+        split(0, 0)
+        cast(nc.vector.tensor_copy, q_bf1[:, halves[1], :], q_raw[1][:, :, halves[1]])
+        for c, o in early[1:]:
+            split(c, o)
         quantize(1, slice(0, NQ), q_bf1[:])
-        for c in range(1, NCH):
-            split(c)
-        for c in range(NCH):
-            for o in range(PASSES):
-                multiply(c, o)
+        nc.vector.tensor_copy(late_keys[:, 0:2, :].bitcast(U16), pairs[:, 1:3, 1, :])
+        nc.vector.tensor_copy(late_keys[:, 2:4, :].bitcast(U16), pairs[:, 3, :, :])
+        for c, o in [(0, 0), (1, 0), (2, 0), (0, 1), (1, 1), (2, 1), (3, 0), (3, 1)]:
+            multiply(c, o)
+
+        bias = shared.tile([P, N], F32, name="bias", offset=3072, align_bytes=64)
+        for h in range(2):
+            nc.scalar.copy(bias[:, h * 2 * CH : (h + 1) * 2 * CH], spread[:, h * 2 * CH : (h + 1) * 2 * CH])
 
         res = sb.tile([P, N], F32, name="res")
         for c in range(NCH):

@@ -26,7 +26,7 @@ ROW_LOW = P - 1
 ROW_HIGH = P - 5
 ROW_STEP = 3
 HALF = T // 2
-SCALAR_ROWS = 96
+SCALAR_ROWS = 80
 GP_START = 96
 FIRST_COLS = 2176
 
@@ -49,7 +49,7 @@ def tile_attend_neu_relu_topk_kernel(tc, qT, k_words, k_scales, nb, offs, out):
         ramp = sb.tile([P, P], F32, name="ramp")
         nc.gpsimd.iota(ramp[:], [[1, P]], base=0, channel_multiplier=-1, allow_small_or_imprecise_dtypes=True)
         ident = sb.tile([P, P], F32, name="ident")
-        dist = shared.tile([P, P], F32, name="dist", offset=6144, align_bytes=64)
+        dist = shared.tile([P, P], F32, name="dist", offset=6400, align_bytes=64)
         nc.scalar.activation(dist[:], ramp[:], ACT.Abs)
         nc.scalar.activation(ident[:], dist[:], ACT.Relu, bias=1.0, scale=-1.0)
 
@@ -66,7 +66,7 @@ def tile_attend_neu_relu_topk_kernel(tc, qT, k_words, k_scales, nb, offs, out):
 
         nc.vector.memset(nb_win[0:ROW_LOW, 0:HALF], 0.0)
 
-        nb_got = [shared.tile([P, N // 2], F32, name="nb_got%d" % h, offset=5120 + 1024 * h, align_bytes=64) for h in range(2)]
+        nb_got = [shared.tile([P, N // 2], F32, name="nb_got%d" % h, offset=5376 + 1024 * h, align_bytes=64) for h in range(2)]
         nc.vector.tensor_copy(nb_got[0][:], nb_win[:].indirect(offsets[:, 0 : N // 32]))
         nc.scalar.activation(nb_got[1][:], nb_win[:].indirect(offsets[:, N // 32 : N // 16]), ACT.Copy)
 
@@ -96,8 +96,8 @@ def tile_attend_neu_relu_topk_kernel(tc, qT, k_words, k_scales, nb, offs, out):
         for c in range(NCH):
             nc.tensor.transpose(spread[:, c * CH : (c + 1) * CH], nb_col[c][:].to_broadcast([P, P]), ident[:])
 
-        q_bf0 = shared.tile([P, NQ, PACK], BF16, name="q_bf0", offset=5632, align_bytes=64)
-        q_bf1 = shared.tile([P, NQ, PACK], BF16, name="q_bf1", offset=6656, align_bytes=64)
+        q_bf0 = shared.tile([P, NQ, PACK], BF16, name="q_bf0", offset=5888, align_bytes=64)
+        q_bf1 = shared.tile([P, NQ, PACK], BF16, name="q_bf1", offset=6912, align_bytes=64)
         q_codes = [sb.tile([P, NQ], U32, name="q_codes%d" % o, align_bytes=64) for o in range(PASSES)]
         q_scales = [sb.tile([P, NQ], U8, name="q_scales%d" % o, align_bytes=64) for o in range(PASSES)]
         halves = [slice(0, SCALAR_ROWS), slice(SCALAR_ROWS, NQ)]
@@ -105,12 +105,14 @@ def tile_attend_neu_relu_topk_kernel(tc, qT, k_words, k_scales, nb, offs, out):
         def cast(copy, grouped, raw):
             copy(grouped.rearrange("p (c i) t -> p c t i", i=4), raw.rearrange("p t (c i) -> p c t i", i=4))
 
-        def round_on_gpsimd(grouped, raw):
-            nc.gpsimd.tensor_scalar(grouped, raw, 1.0, 0.0, ALU.mult, ALU.add)
-
+        cast(nc.vector.tensor_copy, q_bf1[:, halves[1], :], q_raw[1][:, :, halves[1]])
         cast(nc.scalar.copy, q_bf0[:, 0:GP_START, :], q_raw[0][:, :, 0:GP_START])
-        round_on_gpsimd(q_bf0[:, GP_START:NQ, :], q_raw[0][:, :, GP_START:NQ].rearrange("p t w -> p w t"))
+        nc.gpsimd.tensor_scalar(q_bf0[:, GP_START:NQ, :], q_raw[0][:, :, GP_START:NQ].rearrange("p t w -> p w t"), 1.0, 0.0, ALU.mult, ALU.add)
         cast(nc.scalar.copy, q_bf1[:, halves[0], :], q_raw[1][:, :, halves[0]])
+
+        bias = shared.tile([P, N], F32, name="bias", offset=3328, align_bytes=64)
+        for h in range(2):
+            nc.scalar.copy(bias[:, h * 2 * CH : (h + 1) * 2 * CH], spread[:, h * 2 * CH : (h + 1) * 2 * CH])
 
         def quantize(o, rows, grouped):
             nc.vector.quantize_mx(
@@ -119,18 +121,19 @@ def tile_attend_neu_relu_topk_kernel(tc, qT, k_words, k_scales, nb, offs, out):
                 in_=grouped.rearrange("p w j -> p (w j)"),
             )
 
-        early = [(0, 0), (1, 0), (0, 1), (2, 0)]
-        late = [(1, 1), (2, 1), (3, 0), (3, 1)]
-        early_keys = shared.tile([P, 4, 2 * CH], U8, name="early_keys", offset=1024, align_bytes=64)
-        late_keys = shared.tile([P, 4, 2 * CH], U8, name="late_keys", offset=2048, align_bytes=64)
-        keys = {}
-        for i in range(4):
-            keys[early[i]] = early_keys[:, i, :]
-            keys[late[i]] = late_keys[:, i, :]
+        early_keys = shared.tile([P, 3, 2 * CH], U8, name="early_keys", offset=0, align_bytes=64)
+        late_keys = shared.tile([P, 5, 2 * CH], U8, name="late_keys", offset=2048, align_bytes=64)
+        keys = {(0, 0): early_keys[:, 0, :], (1, 0): early_keys[:, 1, :], (0, 1): early_keys[:, 2, :], (1, 1): late_keys[:, 0, :]}
+        for c in (2, 3):
+            for o in range(PASSES):
+                keys[(c, o)] = late_keys[:, 2 * c - 3 + o, :]
         pairs = w_got[:].bitcast(U16).rearrange("p (c n o) -> p c o n", o=PASSES, c=NCH)
 
         def split(c, o):
             nc.vector.tensor_copy(keys[(c, o)].bitcast(U16), pairs[:, c, o, :])
+
+        def split_both(c):
+            nc.vector.tensor_copy(late_keys[:, 2 * c - 3 : 2 * c - 1, :].bitcast(U16), pairs[:, c, :, :])
 
         acc = [ps.tile([P, CH], F32, name="acc%d" % c) for c in range(NCH)]
 
@@ -147,18 +150,14 @@ def tile_attend_neu_relu_topk_kernel(tc, qT, k_words, k_scales, nb, offs, out):
 
         quantize(0, slice(0, NQ), q_bf0[:])
         split(0, 0)
-        cast(nc.vector.tensor_copy, q_bf1[:, halves[1], :], q_raw[1][:, :, halves[1]])
-        for c, o in early[1:]:
-            split(c, o)
+        split(1, 0)
+        split(0, 1)
         quantize(1, slice(0, NQ), q_bf1[:])
-        nc.vector.tensor_copy(late_keys[:, 0:2, :].bitcast(U16), pairs[:, 1:3, 1, :])
-        nc.vector.tensor_copy(late_keys[:, 2:4, :].bitcast(U16), pairs[:, 3, :, :])
-        for c, o in [(0, 0), (1, 0), (2, 0), (0, 1), (1, 1), (2, 1), (3, 0), (3, 1)]:
+        split(1, 1)
+        split_both(2)
+        split_both(3)
+        for c, o in [(0, 0), (1, 0), (0, 1), (1, 1), (2, 0), (2, 1), (3, 0), (3, 1)]:
             multiply(c, o)
-
-        bias = shared.tile([P, N], F32, name="bias", offset=3072, align_bytes=64)
-        for h in range(2):
-            nc.scalar.copy(bias[:, h * 2 * CH : (h + 1) * 2 * CH], spread[:, h * 2 * CH : (h + 1) * 2 * CH])
 
         res = sb.tile([P, N], F32, name="res")
         for c in range(NCH):

@@ -79,15 +79,14 @@ def tile_attend_neu_relu_topk_kernel(tc, qT, k_words, k_scales, nb, offs, out):
             rows = slice(8 * ROW_STEP * quad, 8 * ROW_STEP * (quad + 1), ROW_STEP)
             nc.sync.dma_start(planes_i32[32 * quad : 32 * quad + 4, :, :], sc_got_i32[rows, :])
 
-        nb_low = [sb.tile([P, 2], F32, name="nb_low%d" % h) for h in range(2)]
         nb_col = [sb.tile([P, 1], F32, name="nb_col%d" % c) for c in range(NCH)]
         for h in range(2):
             turned = ps.tile([P, 2, CH], F32, name="turned%d" % h)
             for i in range(2):
                 nc.tensor.transpose(turned[:, i, :], nb_got[h][:, i * CH : (i + 1) * CH], ident[:])
-            nc.scalar.copy(nb_low[h][:], turned[:, :, ROW_LOW])
             for i in range(2):
-                nc.scalar.activation(nb_col[2 * h + i][:], turned[:, i, ROW_HIGH : ROW_HIGH + 1], ACT.Identity, bias=nb_low[h][:, i : i + 1])
+                both = sb.tile([P, 2], F32, name="both%d" % (2 * h + i))
+                nc.scalar.activation(both[:], turned[:, i, ROW_HIGH : ROW_LOW + 1 : ROW_LOW - ROW_HIGH], ACT.Copy, accum_out=nb_col[2 * h + i][:])
 
         w_got = sb.tile([P, N], U32, name="w_got", tag="nb_win", align_bytes=64)
         nc.vector.tensor_copy(w_got[:], w_win[:].bitcast(U32).indirect(offsets[:]))

@@ -24,7 +24,8 @@ CH = 128
 NCH = N // CH
 ROW_LOW = P - 1
 ROW_HIGH = P - 5
-ROW_STEP = 3
+ROW_STEP = 2
+ROW_FIRST = 32
 HALF = T // 2
 SCALAR_ROWS = 80
 GP_START = 96
@@ -58,7 +59,7 @@ def tile_attend_neu_relu_topk_kernel(tc, qT, k_words, k_scales, nb, offs, out):
         sc_win = sb.tile([P, T], U8, name="sc_win", align_bytes=64)
         sc_i32 = sc_win[:].bitcast(I32)
         nc.vector.memset(sc_i32[:], 0)
-        nc.sync.dma_start(sc_i32[0 : 32 * ROW_STEP : ROW_STEP, :], k_scales.rearrange("o f t -> f o t").bitcast(I32))
+        nc.sync.dma_start(sc_i32[ROW_FIRST : ROW_FIRST + 32 * ROW_STEP : ROW_STEP, :], k_scales.rearrange("o f t -> f o t").bitcast(I32))
         nc.sync.dma_start(w_win[:, FIRST_COLS:T], words[:, FIRST_COLS:T])
         q_raw = [shared.tile([P, PACK, NQ], F32, name="q_raw%d" % o, offset=2048 * o, align_bytes=64) for o in range(PASSES)]
         for o in range(PASSES):
@@ -76,7 +77,7 @@ def tile_attend_neu_relu_topk_kernel(tc, qT, k_words, k_scales, nb, offs, out):
         planes_i32 = planes[:].bitcast(I32)
         sc_got_i32 = sc_got[:].bitcast(I32)
         for quad in range(4):
-            rows = slice(8 * ROW_STEP * quad, 8 * ROW_STEP * (quad + 1), ROW_STEP)
+            rows = slice(ROW_FIRST + 8 * ROW_STEP * quad, ROW_FIRST + 8 * ROW_STEP * (quad + 1), ROW_STEP)
             nc.sync.dma_start(planes_i32[32 * quad : 32 * quad + 4, :, :], sc_got_i32[rows, :])
 
         nb_col = [sb.tile([P, 1], F32, name="nb_col%d" % c) for c in range(NCH)]

@@ -23,13 +23,13 @@ PASSES = 2
 CH = 128
 NCH = N // CH
 ROW_LOW = P - 1
-ROW_HIGH = P - 5
+ROW_HIGH = P // 2 - 1
 ROW_STEP = 2
 ROW_FIRST = 32
 HALF = T // 2
 SCALAR_ROWS = 80
 GP_START = 96
-FIRST_COLS = 2176
+FIRST_COLS = 1024
 
 
 def tile_attend_neu_relu_topk_kernel(tc, qT, k_words, k_scales, nb, offs, out):
@@ -43,6 +43,7 @@ def tile_attend_neu_relu_topk_kernel(tc, qT, k_words, k_scales, nb, offs, out):
         nc.sync.dma_start(offsets[:], offs)
         nb_win = sb.tile([P, T], F32, name="nb_win", align_bytes=64)
         nc.sync.dma_start(nb_win[ROW_LOW : ROW_LOW + 1, 0:HALF], nb[0:1, 0:HALF])
+        nc.sync.dma_start(nb_win[ROW_HIGH : ROW_HIGH + 1, HALF:T], nb[0:1, HALF:T])
         w_win = sb.tile([P, T], I32, name="w_win", align_bytes=64)
         words = k_words[0].rearrange("p t b -> p (t b)").bitcast(I32)
         nc.scalar.dma_start(w_win[:, 0:FIRST_COLS], words[:, 0:FIRST_COLS])
@@ -54,8 +55,6 @@ def tile_attend_neu_relu_topk_kernel(tc, qT, k_words, k_scales, nb, offs, out):
         nc.scalar.activation(dist[:], ramp[:], ACT.Abs)
         nc.scalar.activation(ident[:], dist[:], ACT.Relu, bias=1.0, scale=-1.0)
 
-        nc.vector.memset(nb_win[:, HALF:T], 0.0)
-        nc.sync.dma_start(nb_win[ROW_HIGH : ROW_HIGH + 1, HALF:T], nb[0:1, HALF:T])
         sc_win = sb.tile([P, T], U8, name="sc_win", align_bytes=64)
         sc_i32 = sc_win[:].bitcast(I32)
         nc.vector.memset(sc_i32[:], 0)
@@ -66,6 +65,8 @@ def tile_attend_neu_relu_topk_kernel(tc, qT, k_words, k_scales, nb, offs, out):
             nc.sync.dma_start(q_raw[o][:], qT[0, 512 * o : 512 * (o + 1), :].rearrange("(p j) w -> p j w", j=PACK))
 
         nc.vector.memset(nb_win[0:ROW_LOW, 0:HALF], 0.0)
+        nc.vector.memset(nb_win[0:ROW_HIGH, HALF:T], 0.0)
+        nc.vector.memset(nb_win[ROW_HIGH + 1 : P, HALF:T], 0.0)
 
         nb_got = [shared.tile([P, N // 2], F32, name="nb_got%d" % h, offset=5376 + 1024 * h, align_bytes=64) for h in range(2)]
         nc.vector.tensor_copy(nb_got[0][:], nb_win[:].indirect(offsets[:, 0 : N // 32]))

@@ -40,10 +40,10 @@ def tile_attend_neu_relu_topk_kernel(tc, qT, k_words, k_scales, nb, offs, out):
         ps = ctx.enter_context(tc.psum_pool(name="ps", bufs=1))
 
         offsets = sb.tile([P, N // 16], U16, name="offsets")
-        nc.sync.dma_start(offsets[:], offs)
         nb_win = sb.tile([P, T], F32, name="nb_win", align_bytes=64)
         nc.sync.dma_start(nb_win[ROW_LOW : ROW_LOW + 1, 0:HALF], nb[0:1, 0:HALF])
         nc.sync.dma_start(nb_win[ROW_HIGH : ROW_HIGH + 1, HALF:T], nb[0:1, HALF:T])
+        nc.sync.dma_start(offsets[:], offs)
         w_win = sb.tile([P, T], I32, name="w_win", align_bytes=64)
         words = k_words[0].rearrange("p t b -> p (t b)").bitcast(I32)
         nc.scalar.dma_start(w_win[:, 0:FIRST_COLS], words[:, 0:FIRST_COLS])

from contextlib import ExitStack

import concourse.mybir as mybir

D, NQ, T, N = 1024, 128, 4096, 512
FLOPS = 2 * D * NQ * N
BYTES = D * NQ * 4 + 128 * T * 4 + 32 * T + T * 4 + 128 * 32 * 2 + NQ * N * 4

F32 = mybir.dt.float32
BF16 = mybir.dt.bfloat16
I32 = mybir.dt.int32
U32 = mybir.dt.uint32
U16 = mybir.dt.uint16
U8 = mybir.dt.uint8
FP8X4 = mybir.dt.float8_e4m3fn_x4
FP4X4 = mybir.dt.float4_e2m1fn_x4
ACT = mybir.ActivationFunctionType
ALU = mybir.AluOpType

P = 128
PACK = 4
PASSES = 2
CH = 128
NCH = N // CH
ROW_LOW = P - 1
ROW_HIGH = P // 2 - 1
ROW_STEP = 2
ROW_FIRST = 32
HALF = T // 2
SCALAR_ROWS = 80
GP_START = 96
FIRST_COLS = 1024


def tile_attend_neu_relu_topk_kernel(tc, qT, k_words, k_scales, nb, offs, out):
    nc = tc.nc
    with ExitStack() as ctx:
        sb = ctx.enter_context(tc.tile_pool(name="sb", bufs=1))
        shared = ctx.enter_context(tc.tile_pool(name="shared", bufs=1))
        ps = ctx.enter_context(tc.psum_pool(name="ps", bufs=1))

        offsets = sb.tile([P, N // 16], U16, name="offsets")
        nb_win = sb.tile([P, T], F32, name="nb_win", align_bytes=64)
        nc.sync.dma_start(nb_win[ROW_LOW : ROW_LOW + 1, 0:HALF], nb[0:1, 0:HALF])
        nc.sync.dma_start(nb_win[ROW_HIGH : ROW_HIGH + 1, HALF:T], nb[0:1, HALF:T])
        nc.sync.dma_start(offsets[:], offs)
        w_win = sb.tile([P, T], I32, name="w_win", align_bytes=64)
        words = k_words[0].rearrange("p t b -> p (t b)").bitcast(I32)
        nc.scalar.dma_start(w_win[:, 0:FIRST_COLS], words[:, 0:FIRST_COLS])

        ramp = sb.tile([P, P], F32, name="ramp")
        nc.gpsimd.iota(ramp[:], [[1, P]], base=0, channel_multiplier=-1, allow_small_or_imprecise_dtypes=True)
        ident = sb.tile([P, P], F32, name="ident")
        dist = shared.tile([P, P], F32, name="dist", offset=6400, align_bytes=64)
        nc.scalar.activation(dist[:], ramp[:], ACT.Abs)
        nc.scalar.activation(ident[:], dist[:], ACT.Relu, bias=1.0, scale=-1.0)

        sc_win = sb.tile([P, T], U8, name="sc_win", align_bytes=64)
        sc_i32 = sc_win[:].bitcast(I32)
        nc.vector.memset(sc_i32[:], 0)
        nc.sync.dma_start(sc_i32[ROW_FIRST : ROW_FIRST + 32 * ROW_STEP : ROW_STEP, :], k_scales.rearrange("o f t -> f o t").bitcast(I32))
        nc.sync.dma_start(w_win[:, FIRST_COLS:T], words[:, FIRST_COLS:T])
        q_raw = [shared.tile([P, PACK, NQ], F32, name="q_raw%d" % o, offset=2048 * o, align_bytes=64) for o in range(PASSES)]
        for o in range(PASSES):
            nc.sync.dma_start(q_raw[o][:], qT[0, 512 * o : 512 * (o + 1), :].rearrange("(p j) w -> p j w", j=PACK))

        nc.vector.memset(nb_win[0:ROW_LOW, 0:HALF], 0.0)
        nc.vector.memset(nb_win[0:ROW_HIGH, HALF:T], 0.0)
        nc.vector.memset(nb_win[ROW_HIGH + 1 : P, HALF:T], 0.0)

        nb_got = [shared.tile([P, N // 2], F32, name="nb_got%d" % h, offset=5376 + 1024 * h, align_bytes=64) for h in range(2)]
        nc.vector.tensor_copy(nb_got[0][:], nb_win[:].indirect(offsets[:, 0 : N // 32]))
        nc.scalar.activation(nb_got[1][:], nb_win[:].indirect(offsets[:, N // 32 : N // 16]), ACT.Copy)

        sc_got = sb.tile([P, N], U8, name="sc_got", align_bytes=64)
        nc.vector.tensor_copy(sc_got[:], sc_win[:].indirect(offsets[:]))
        planes = sb.tile([P, PASSES, N], U8, name="planes", align_bytes=64)
        planes_i32 = planes[:].bitcast(I32)
        sc_got_i32 = sc_got[:].bitcast(I32)
        for quad in range(4):
            rows = slice(ROW_FIRST + 8 * ROW_STEP * quad, ROW_FIRST + 8 * ROW_STEP * (quad + 1), ROW_STEP)
            nc.sync.dma_start(planes_i32[32 * quad : 32 * quad + 4, :, :], sc_got_i32[rows, :])

        nb_col = [sb.tile([P, 1], F32, name="nb_col%d" % c) for c in range(NCH)]
        for h in range(2):
            turned = ps.tile([P, 2, CH], F32, name="turned%d" % h)
            for i in range(2):
                nc.tensor.transpose(turned[:, i, :], nb_got[h][:, i * CH : (i + 1) * CH], ident[:])
            for i in range(2):
                both = sb.tile([P, 2], F32, name="both%d" % (2 * h + i))
                nc.scalar.activation(both[:], turned[:, i, ROW_HIGH : ROW_LOW + 1 : ROW_LOW - ROW_HIGH], ACT.Copy, accum_out=nb_col[2 * h + i][:])

        w_got = sb.tile([P, N], U32, name="w_got", tag="nb_win", align_bytes=64)
        nc.vector.tensor_copy(w_got[:], w_win[:].bitcast(U32).indirect(offsets[:]))

        spread = ps.tile([P, N], F32, name="spread")
        for c in range(NCH):
            nc.tensor.transpose(spread[:, c * CH : (c + 1) * CH], nb_col[c][:].to_broadcast([P, P]), ident[:])

        q_bf0 = shared.tile([P, NQ, PACK], BF16, name="q_bf0", offset=5888, align_bytes=64)
        q_bf1 = shared.tile([P, NQ, PACK], BF16, name="q_bf1", offset=6912, align_bytes=64)
        q_codes = [sb.tile([P, NQ], U32, name="q_codes%d" % o, align_bytes=64) for o in range(PASSES)]
        q_scales = [sb.tile([P, NQ], U8, name="q_scales%d" % o, align_bytes=64) for o in range(PASSES)]
        halves = [slice(0, SCALAR_ROWS), slice(SCALAR_ROWS, NQ)]

        def cast(copy, grouped, raw):
            copy(grouped.rearrange("p (c i) t -> p c t i", i=4), raw.rearrange("p t (c i) -> p c t i", i=4))

        cast(nc.vector.tensor_copy, q_bf1[:, halves[1], :], q_raw[1][:, :, halves[1]])
        cast(nc.scalar.copy, q_bf0[:, 0:GP_START, :], q_raw[0][:, :, 0:GP_START])
        nc.gpsimd.tensor_scalar(q_bf0[:, GP_START:NQ, :], q_raw[0][:, :, GP_START:NQ].rearrange("p t w -> p w t"), 1.0, 0.0, ALU.mult, ALU.add)
        cast(nc.scalar.copy, q_bf1[:, halves[0], :], q_raw[1][:, :, halves[0]])

        bias = shared.tile([P, N], F32, name="bias", offset=3328, align_bytes=64)
        for h in range(2):
            nc.scalar.copy(bias[:, h * 2 * CH : (h + 1) * 2 * CH], spread[:, h * 2 * CH : (h + 1) * 2 * CH])

        def quantize(o, rows, grouped):
            nc.vector.quantize_mx(
                out=q_codes[o][:, rows].bitcast(FP8X4),
                scales=q_scales[o][:, rows],
                in_=grouped.rearrange("p w j -> p (w j)"),
            )

        early_keys = shared.tile([P, 3, 2 * CH], U8, name="early_keys", offset=0, align_bytes=64)
        late_keys = shared.tile([P, 5, 2 * CH], U8, name="late_keys", offset=2048, align_bytes=64)
        keys = {(0, 0): early_keys[:, 0, :], (1, 0): early_keys[:, 1, :], (0, 1): early_keys[:, 2, :], (1, 1): late_keys[:, 0, :]}
        for c in (2, 3):
            for o in range(PASSES):
                keys[(c, o)] = late_keys[:, 2 * c - 3 + o, :]
        pairs = w_got[:].bitcast(U16).rearrange("p (c n o) -> p c o n", o=PASSES, c=NCH)

        def split(c, o):
            nc.vector.tensor_copy(keys[(c, o)].bitcast(U16), pairs[:, c, o, :])

        def split_both(c):
            nc.vector.tensor_copy(late_keys[:, 2 * c - 3 : 2 * c - 1, :].bitcast(U16), pairs[:, c, :, :])

        acc = [ps.tile([P, CH], F32, name="acc%d" % c) for c in range(NCH)]

        def multiply(c, o):
            nc.tensor.matmul_mx(
                out=acc[c][:],
                lhsT=q_codes[o][:].bitcast(FP8X4),
                lhsT_scale=q_scales[o][:],
                rhs=keys[(c, o)].bitcast(FP4X4),
                rhs_scale=planes[:, o, c * CH : (c + 1) * CH],
                start=(o == 0),
                stop=(o == PASSES - 1),
            )

        quantize(0, slice(0, NQ), q_bf0[:])
        split(0, 0)
        split(1, 0)
        split(0, 1)
        quantize(1, slice(0, NQ), q_bf1[:])
        split(1, 1)
        split_both(2)
        split_both(3)
        for c, o in [(0, 0), (1, 0), (0, 1), (1, 1), (2, 0), (2, 1), (3, 0), (3, 1)]:
            multiply(c, o)

        res = sb.tile([P, N], F32, name="res")
        for c in range(NCH):
            cols = slice(c * CH, (c + 1) * CH)
            summed = sb.tile([P, CH], F32, name="summed%d" % c)
            nc.vector.tensor_tensor(summed[:], acc[c][:], bias[:, cols], ALU.add)
            if c < NCH - 1:
                nc.scalar.activation(res[:, cols], summed[:], ACT.Relu)
            else:
                nc.vector.tensor_scalar_max(res[:, cols], summed[:], 0.0)
            queue = nc.scalar if c == NCH - 2 else nc.sync
            queue.dma_start(out[0, :, cols], res[:, cols])
